import numpy as np
import ml_dtypes


def mxq(x, axis, fmt="e4m3"):
    dtype, down = {"e4m3": (ml_dtypes.float8_e4m3fn, 7), "e5m2": (ml_dtypes.float8_e5m2, 14)}[fmt]
    v = np.moveaxis(np.asarray(x, np.float32).astype(ml_dtypes.bfloat16).astype(np.float64), axis, -1)
    blocks = v.reshape(v.shape[:-1] + (-1, 32))
    amax = np.abs(blocks).max(-1, keepdims=True)
    byte = np.maximum(np.where(amax > 0, np.frexp(amax)[1] - 1 + 127, 0) - down, 1)
    scale = np.exp2(byte - 127.0)
    codes = (blocks / scale).astype(np.float32).astype(dtype).astype(np.float64)
    return np.moveaxis((codes * scale).reshape(v.shape), -1, axis)


WIDE = False


def mx_kscale(k):
    if not WIDE:
        return np.ones(k)
    levels = np.array([10, -10, 5, -5, 0])
    if k % 512:
        return np.exp2(np.random.permutation(np.resize(levels, k // 32))).repeat(32)
    a = np.empty((k // 512, 16))
    for p in range(k // 512):
        a[p, :8] = np.random.permutation(np.resize(levels, 8))
        for g in range(8):
            far = levels[np.abs(levels - a[p, g]) >= 10]
            a[p, g + 8] = far[np.random.randint(len(far))]
    return np.exp2(a.ravel()).repeat(32)


def f64(x):
    return np.asarray(x).astype(np.float64)


def striped(idx):
    return np.tile(np.asarray(idx).reshape(-1, 16).T, (8, 1)).astype(np.uint16)


def unstriped(offs):
    return offs[:16].T.reshape(-1).astype(np.int64)


E2M1 = np.array([0.0, 0.5, 1.0, 1.5, 2.0, 3.0, 4.0, 6.0, -0.0, -0.5, -1.0, -1.5, -2.0, -3.0, -4.0, -6.0])


def pack_weight(w, fmt):
    k, n = w.shape
    w = f64(np.asarray(w, np.float32).astype(ml_dtypes.bfloat16)).reshape(k // 32, 32, n)
    amax = np.abs(w).max(1)
    if fmt == "e4m3":
        byte = np.frexp(amax)[1] - 1 + 127 - 7
    else:
        mant, ex = np.frexp(amax / 6.0)
        byte = np.where(mant > 0.5, ex, ex - 1) + 127
    byte = np.clip(np.where(amax > 0, byte, 1), 1, 254)
    scaled = (w * np.exp2(127.0 - byte)[:, None, :]).reshape(k, n).astype(np.float32)
    by_word = np.ascontiguousarray(scaled.reshape(k // 512, 128, 4, n).transpose(0, 1, 3, 2))
    if fmt == "e4m3":
        words = by_word.astype(ml_dtypes.float8_e4m3fn).view(np.uint8)
    else:
        c = by_word.astype(ml_dtypes.float4_e2m1fn).view(np.uint8) & 0xF
        words = (c[..., 0::2] | (c[..., 1::2] << 4)).reshape(k // 512, 128, 2 * n)
    return np.ascontiguousarray(words), np.ascontiguousarray(byte.astype(np.uint8).reshape(k // 512, 16, n))


def unpack_weight(words, scales, fmt):
    g, _, n = scales.shape
    words = np.ascontiguousarray(words).reshape(g, 128, n, -1)
    if fmt == "e4m3":
        vals = words.view(ml_dtypes.float8_e4m3fn).astype(np.float64)
    else:
        nib = np.empty((g, 128, n, 4), np.uint8)
        nib[..., 0::2] = words & 0xF
        nib[..., 1::2] = words >> 4
        vals = E2M1[nib]
    vals = vals * np.repeat(np.exp2(scales.astype(np.float64) - 127.0), 8, axis=1)[..., None]
    return vals.transpose(0, 1, 3, 2).reshape(g * 512, n)


def bf(x):
    return np.asarray(x, np.float32).astype(ml_dtypes.bfloat16)


def planes(Y):
    r, m = Y.shape
    b = f64(bf(Y)).reshape(r // 32, 32, m)
    amax = np.abs(b).max(1)
    byte = np.clip(np.where(amax > 0, np.frexp(amax)[1] - 1 + 127 - 7, 1), 1, 254)
    codes = (b * np.exp2(127.0 - byte)[:, None, :]).reshape(r, m).astype(np.float32).astype(ml_dtypes.float8_e4m3fn).view(np.uint8)
    words = codes.reshape(r // 512, 128, 4, m).transpose(0, 1, 3, 2)
    return np.ascontiguousarray(words), np.ascontiguousarray(byte.astype(np.uint8).reshape(r // 512, 16, m))


D, T, I, Q, E, U = 512, 2048, 512, 256, 512, 1024


def setup_inputs():
    n = np.random.standard_normal
    idx = np.random.permutation(T)[:I]
    idx2 = np.random.permutation(U)[:I]
    idx4 = np.random.permutation(I)[:I]
    fd = mx_kscale(D)
    fi = mx_kscale(I)
    ti = np.ones(T)
    ti[idx] = fi
    keysp = pack_weight(n((D, T)) / fd[:, None], "e2m1")
    return {
        "query": (n((D, Q)) * 0.9 / np.sqrt(D) * fd[:, None]).astype(np.float32),
        "keys_words": keysp[0],
        "keys_scales": keysp[1],
        "query2": (n((D, Q)) * 0.9 / np.sqrt(D) * fd[:, None]).astype(np.float32),
        "notes": (n((D, U)) / fd[:, None]).astype(np.float32),
        "lam": (np.random.uniform(0.1, 0.5, (Q, 1))).astype(np.float32),
        "rival": (np.random.uniform(0.5, 2.0, (Q, 1))).astype(np.float32),
        "os": (np.random.uniform(4.0, 16.0, (1, I)) * fi).astype(np.float32),
        "vals": (n((E, T)) / ti).astype(np.float32),
        "before": (n((E, Q))).astype(np.float32),
        "hold": (np.random.uniform(0.1, 0.6, (1, Q))).astype(np.float32),
        "offs": striped(idx),
        "offs2": striped(idx2),
        "offs4": striped(idx4),
    }


def reference(query, keys_words, keys_scales, query2, notes, lam, rival, os, vals, before, hold, offs, offs2, offs4):
    idx = unstriped(offs)
    idx2 = unstriped(offs2)
    idx4 = unstriped(offs4)
    keysu = unpack_weight(keys_words, keys_scales, "e2m1")
    queryq = mxq(f64(query), 0, "e4m3")
    keysidxg = keysu[:, idx]
    a = queryq.T @ keysidxg
    query2q = mxq(f64(query2), 0, "e4m3")
    notesidx2q = mxq(f64(notes)[:, idx2], 0, "e4m3")
    b = query2q.T @ notesidx2q
    s = np.maximum(a, b) + np.minimum(a, b) * f64(lam)
    p = np.exp(s)
    r = p / (p + p[:, idx4] * f64(rival))
    w = r / np.sum(r, axis=1, keepdims=True)
    wo1 = w * f64(os)
    wt1 = wo1.T
    vt1 = f64(vals)[:, idx].T
    vt1q = mxq(vt1, 0, "e4m3")
    wt1q = mxq(wt1, 0, "e4m3")
    o = vt1q.T @ wt1q
    y = f64(before) * f64(hold) + o * (1.0 - f64(hold))
    words, scales = planes(y)
    return y, words, scales

@@ -1,0 +1,273 @@
+from contextlib import ExitStack
+
+import concourse.mybir as mybir
+from concourse.masks import make_identity
+
+F32 = mybir.dt.float32
+BF16 = mybir.dt.bfloat16
+I32 = mybir.dt.int32
+U32 = mybir.dt.uint32
+U16 = mybir.dt.uint16
+U8 = mybir.dt.uint8
+FP8X4 = mybir.dt.float8_e4m3fn_x4
+FP4X4 = mybir.dt.float4_e2m1fn_x4
+ALU = mybir.AluOpType
+ACT = mybir.ActivationFunctionType
+
+D, T, I, Q, E, U = 512, 2048, 512, 256, 512, 1024
+P = 128
+PACK = 4
+QT = Q // P
+HALF = I // 2
+LIST_COLS = I // 16
+
+FLOPS = 2 * D * Q * I * 2 + 2 * I * E * Q
+
+
+def tile_attend_twopools_overlinked_blend_pl_kernel(
+    tc, query, keys_words, keys_scales, query2, notes, lam, rival, slot_factor, vals, before, hold,
+    offs, offs2, offs4, out_0, out_1, out_2,
+):
+    nc = tc.nc
+    with ExitStack() as ctx:
+        sb = ctx.enter_context(tc.tile_pool(name="sb", bufs=1))
+        ps = ctx.enter_context(tc.psum_pool(name="ps", bufs=1))
+
+        def sbuf(name, shape, dtype):
+            return sb.tile(shape, dtype, name=name, align_bytes=64)
+
+        def bank(tag, shape):
+            return ps.tile(shape, F32, name=tag, tag=tag)
+
+        def half_list(lst, h):
+            return lst[:, h * LIST_COLS // 2 : (h + 1) * LIST_COLS // 2]
+
+        key_list = sbuf("key_list", [P, LIST_COLS], U16)
+        note_list = sbuf("note_list", [P, LIST_COLS], U16)
+        rival_list = sbuf("rival_list", [P, LIST_COLS], U16)
+
+        key_scale_pool = sbuf("key_scale_pool", [P, T], U8)
+        nc.vector.memset(key_scale_pool[:].bitcast(I32), 0)
+        ident = sbuf("ident", [P, P], F32)
+        make_identity(nc, ident[:])
+
+        vec_rows = sbuf("vec_rows", [P, P], F32)
+        nc.gpsimd.memset(vec_rows[:], 0.0)
+        one = sbuf("one", [P, 1], F32)
+        nc.gpsimd.memset(one[:], 1.0)
+        mean_factors = sbuf("mean_factors", [P, 2], F32)
+        nc.gpsimd.memset(mean_factors[:, 0:1], -1.0 / I)
+        nc.gpsimd.memset(mean_factors[:, 1:2], 1.0 / I)
+
+        note_planes = notes.rearrange("(p t) u -> p t u", t=PACK)
+        val_planes = vals.rearrange("(p t) n -> p t n", t=PACK)
+        note_pool = [sbuf("note_pool%d" % t, [P, U], F32) for t in range(PACK)]
+        val_pool = [sbuf("val_pool%d" % t, [P, T], F32) for t in range(PACK)]
+        key_word_pool = sbuf("key_word_pool", [P, T], U16)
+        q_raw = sbuf("q_raw", [P, PACK, Q], F32)
+        q2_raw = sbuf("q2_raw", [P, PACK, Q], F32)
+        before_sb = sbuf("before_sb", [P, PACK, Q], F32)
+
+        nc.sync.dma_start(note_list[:], offs2)
+        nc.sync.dma_start(out=note_pool[0][:], in_=note_planes[:, 0, :])
+        nc.sync.dma_start(out=note_pool[1][:], in_=note_planes[:, 1, :])
+        for quad in range(4):
+            nc.sync.dma_start(
+                out=key_scale_pool[32 * quad : 32 * quad + 4, :].bitcast(I32),
+                in_=keys_scales[0, 4 * quad : 4 * quad + 4, :].bitcast(I32),
+            )
+        nc.sync.dma_start(key_list[:], offs)
+        for t in range(2, PACK):
+            nc.sync.dma_start(out=note_pool[t][:], in_=note_planes[:, t, :])
+        nc.sync.dma_start(out=vec_rows[0:2, :], in_=lam.rearrange("(j p) o -> j (p o)", p=P))
+        nc.sync.dma_start(out=vec_rows[2:4, :], in_=rival.rearrange("(j p) o -> j (p o)", p=P))
+        nc.sync.dma_start(out=vec_rows[4:6, :], in_=hold.rearrange("o (j p) -> j (o p)", p=P))
+        nc.sync.dma_start(out=vec_rows[8:12, :], in_=slot_factor.rearrange("o (j p) -> j (o p)", p=P))
+        nc.sync.dma_start(out=key_word_pool[:].bitcast(I32), in_=keys_words[0].bitcast(I32))
+        nc.sync.dma_start(out=q_raw[:], in_=query.rearrange("(p t) q -> p t q", t=PACK))
+        nc.sync.dma_start(out=q2_raw[:], in_=query2.rearrange("(p t) q -> p t q", t=PACK))
+        nc.sync.dma_start(rival_list[:], offs4)
+        for t in range(PACK):
+            nc.sync.dma_start(out=val_pool[t][:], in_=val_planes[:, t, :])
+        nc.sync.dma_start(out=before_sb[:], in_=before.rearrange("(p t) q -> p t q", t=PACK))
+
+
+        notes_g = sbuf("notes_g", [P, PACK, I], BF16)
+        nc.scalar.activation(notes_g[:, 0, :], note_pool[0][:].indirect(note_list[:]), ACT.Copy)
+        nc.vector.tensor_copy(notes_g[:, 1, :], note_pool[1][:].indirect(note_list[:]))
+        key_scales = sbuf("key_scales", [P, I], U8)
+        nc.vector.tensor_copy(key_scales[:], key_scale_pool[:].indirect(key_list[:]))
+        nc.scalar.activation(notes_g[:, 2, :], note_pool[2][:].indirect(note_list[:]), ACT.Copy)
+        nc.vector.tensor_copy(notes_g[:, 3, 0:HALF], note_pool[3][:].indirect(half_list(note_list, 0)))
+        nc.scalar.activation(notes_g[:, 3, HALF:I], note_pool[3][:].indirect(half_list(note_list, 1)), ACT.Copy)
+        vec_ps = bank("turn0", [P, P])
+        nc.tensor.transpose(vec_ps[:], vec_rows[:], ident[:])
+        vec = sbuf("vec", [P, 12], F32)
+        nc.vector.tensor_copy(out=vec[:], in_=vec_ps[:, 0:12])
+        lam_col = [vec[:, j : j + 1] for j in range(QT)]
+        rival_col = [vec[:, 2 + j : 3 + j] for j in range(QT)]
+        hold_ps = bank("turn1", [P, QT, P])
+        for j in range(QT):
+            nc.tensor.transpose(hold_ps[:, j, :], vec[:, 4 + j : 5 + j].to_broadcast([P, P]), ident[:])
+        os_ps = bank("factor", [P, I // P, P])
+        for c in range(I // P):
+            nc.tensor.transpose(os_ps[:, c, :], vec[:, 8 + c : 9 + c].to_broadcast([P, P]), ident[:])
+        hold_row = sbuf("hold_row", [P, Q], F32)
+        rest_row = sbuf("rest_row", [P, Q], F32)
+        notes_b = sbuf("notes_b", [P, I, PACK], BF16)
+        notes_t = notes_g[:].rearrange("p t i -> p i t")
+        nc.vector.tensor_copy(out=notes_b[:, 0:HALF, :], in_=notes_t[:, 0:HALF, :])
+        nc.scalar.copy(out=notes_b[:, HALF:I, :], in_=notes_t[:, HALF:I, :])
+        key_words = sbuf("key_words", [P, I], U16)
+        nc.vector.tensor_copy(key_words[:], key_word_pool[:].indirect(key_list[:]))
+        note_codes = sbuf("note_codes", [P, I], U32)
+        note_scales = sbuf("note_scales", [P, I], U8)
+        nc.vector.quantize_mx(out=note_codes[:].bitcast(FP8X4), scales=note_scales[:],
+                              in_=notes_b[:].rearrange("p i t -> p (i t)"))
+
+        q_b = sbuf("q_b", [P, Q, PACK], BF16)
+        q2_b = [sbuf("q2_b%d" % j, [P, P, PACK], BF16) for j in range(QT)]
+        nc.scalar.copy(out=q_b[:], in_=q_raw[:].rearrange("p t q -> p q t"))
+        q2_t = q2_raw[:].rearrange("p t q -> p q t")
+        nc.vector.tensor_copy(out=q2_b[0][:], in_=q2_t[:, 0:P, :])
+        nc.scalar.copy(out=q2_b[1][:], in_=q2_t[:, P:Q, :])
+        q_codes = sbuf("q_codes", [P, Q], U32)
+        q_scales = sbuf("q_scales", [P, Q], U8)
+        nc.vector.quantize_mx(out=q_codes[:].bitcast(FP8X4), scales=q_scales[:],
+                              in_=q_b[:].rearrange("p q t -> p (q t)"))
+        q2_codes = [sbuf("q2_codes%d" % j, [P, P], U32) for j in range(QT)]
+        q2_scales = [sbuf("q2_scales%d" % j, [P, P], U8) for j in range(QT)]
+        for j in range(QT):
+            nc.vector.quantize_mx(out=q2_codes[j][:].bitcast(FP8X4), scales=q2_scales[j][:],
+                                  in_=q2_b[j][:].rearrange("p q t -> p (q t)"))
+
+        a_ps, b_ps, a_sb = [], [], []
+        for j in range(QT):
+            cols = slice(j * P, (j + 1) * P)
+            a_ps.append(bank("first%d" % j, [P, I]))
+            b_ps.append(bank("second%d" % j, [P, I]))
+            nc.tensor.matmul_mx(out=a_ps[j][:], lhsT=q_codes[:, cols].bitcast(FP8X4), lhsT_scale=q_scales[:, cols],
+                                rhs=key_words[:].bitcast(FP4X4), rhs_scale=key_scales[:], start=True, stop=True)
+            nc.tensor.matmul_mx(out=b_ps[j][:], lhsT=q2_codes[j][:].bitcast(FP8X4), lhsT_scale=q2_scales[j][:],
+                                rhs=note_codes[:].bitcast(FP8X4), rhs_scale=note_scales[:], start=True, stop=True)
+            a_sb.append(sbuf("a_sb%d" % j, [P, I], F32))
+            nc.scalar.copy(out=a_sb[j][:], in_=a_ps[j][:])
+
+        nc.scalar.copy(out=hold_row[:], in_=hold_ps[:].rearrange("p j q -> p (j q)"))
+        nc.gpsimd.tensor_scalar(rest_row[:], hold_row[:], -1.0, 1.0, ALU.mult, ALU.add)
+        val_codes = [sbuf("val_codes%d" % t, [P, P], U32) for t in range(PACK)]
+        val_scales = [sbuf("val_scales%d" % t, [P, P], U8) for t in range(PACK)]
+        vals_g = [sbuf("vals_g%d" % t, [P, I], BF16) for t in range(PACK)]
+        vals_b = [sbuf("vals_b%d" % t, [P, P, PACK], BF16) for t in range(PACK)]
+
+        def turn(src, tag, dst):
+            words = src[:].bitcast(F32)
+            turned = bank(tag, [P, 2, P])
+            for u in range(2):
+                nc.tensor.transpose(turned[:, u, :], words[:, u : I // 2 : 2], ident[:])
+            nc.scalar.copy(
+                out=dst[:].rearrange("p c t -> p (c t)").bitcast(F32).rearrange("p (c u) -> p c u", u=2),
+                in_=turned[:].rearrange("p u c -> p c u"))
+
+        def gather_vals(t):
+            nc.scalar.activation(vals_g[t][:], val_pool[t][:].indirect(key_list[:]), ACT.Copy)
+            turn(vals_g[t], "turn%d" % (t % 3), vals_b[t])
+
+        def quantize_vals(t):
+            nc.vector.quantize_mx(out=val_codes[t][:].bitcast(FP8X4), scales=val_scales[t][:],
+                                  in_=vals_b[t][:].rearrange("p c t -> p (c t)"))
+
+        p_sb, p_inv = [], []
+        for j in range(QT):
+            low = sbuf("low%d" % j, [P, I], F32)
+            high = sbuf("high%d" % j, [P, I], F32)
+            s = sbuf("s%d" % j, [P, I], F32)
+            s_sum = sbuf("s_sum%d" % j, [P, 1], F32)
+            nc.vector.tensor_tensor(low[:], a_sb[j][:], b_ps[j][:], ALU.min)
+            nc.vector.tensor_tensor(high[:], a_sb[j][:], b_ps[j][:], ALU.max)
+            nc.vector.scalar_tensor_tensor(s[:], low[:], lam_col[j], high[:], ALU.mult, ALU.add, accum_out=s_sum[:])
+            if j == 0:
+                gather_vals(0)
+            mean = sbuf("mean%d" % j, [P, 2], F32)
+            nc.scalar.activation(mean[:], mean_factors[:], ACT.Copy, scale=s_sum[:])
+            p_sb.append(sbuf("p%d" % j, [P, I], F32))
+            p_inv.append(sbuf("p_inv%d" % j, [P, I], F32))
+            nc.scalar.activation(p_sb[j][:], s[:], ACT.Exp, bias=mean[:, 0:1])
+            nc.scalar.activation(p_inv[j][:], s[:], ACT.Exp, bias=mean[:, 1:2], scale=-1.0)
+
+        ratio, positive = [], []
+        for j in range(QT):
+            ratio.append(sbuf("ratio%d" % j, [P, I], F32))
+            for h in range(2):
+                cols = slice(h * HALF, (h + 1) * HALF)
+                nc.vector.tensor_tensor(ratio[j][:, cols], p_sb[j][:].indirect(half_list(rival_list, h)),
+                                        p_inv[j][:, cols], ALU.mult)
+        quantize_vals(0)
+        size = []
+        for j in range(QT):
+            positive.append(sbuf("positive%d" % j, [P, I], F32))
+            nc.vector.tensor_scalar(positive[j][:], ratio[j][:], rival_col[j], -1.0, ALU.mult, ALU.is_ge)
+            root = sbuf("root%d" % j, [P, I], F32)
+            nc.scalar.activation(root[:], ratio[j][:], ACT.Abs_reciprocal_sqrt, bias=one[:], scale=rival_col[j])
+            size.append(sbuf("size%d" % j, [P, I], F32))
+            nc.scalar.activation(size[j][:], root[:], ACT.Square)
+
+        w_b, w_bf = [], []
+        for j in range(QT):
+            part = sbuf("part%d" % j, [P, I], F32)
+            part_sum = sbuf("part_sum%d" % j, [P, 1], F32)
+            part_inv = sbuf("part_inv%d" % j, [P, 1], F32)
+            nc.vector.scalar_tensor_tensor(part[:], positive[j][:], 0.5, size[j][:], ALU.subtract, ALU.mult,
+                                           accum_out=part_sum[:])
+            nc.vector.reciprocal(part_inv[:], part_sum[:])
+            w_bf.append(sbuf("w_bf%d" % j, [P, I], BF16))
+            nc.vector.scalar_tensor_tensor(w_bf[j][:], part[:], part_inv[:], os_ps[:].rearrange("p c i -> p (c i)"),
+                                           ALU.mult, ALU.mult)
+            w_b.append(sbuf("w_b%d" % j, [P, P, PACK], BF16))
+        gather_vals(1)
+        turn(w_bf[0], "second0", w_b[0])
+        gather_vals(2)
+        turn(w_bf[1], "second1", w_b[1])
+        gather_vals(3)
+        kept = sbuf("kept", [P, PACK, Q], F32)
+        nc.vector.tensor_tensor(kept[:], before_sb[:], hold_row[:].unsqueeze(1).to_broadcast([P, PACK, Q]), ALU.mult)
+        w_codes = [sbuf("w_codes%d" % j, [P, P], U32) for j in range(QT)]
+        w_scales = [sbuf("w_scales%d" % j, [P, P], U8) for j in range(QT)]
+
+        def quantize_w(j):
+            nc.vector.quantize_mx(out=w_codes[j][:].bitcast(FP8X4), scales=w_scales[j][:],
+                                  in_=w_b[j][:].rearrange("p c t -> p (c t)"))
+
+        quantize_vals(1)
+        quantize_w(0)
+        quantize_vals(2)
+        quantize_w(1)
+        quantize_vals(3)
+
+        y_words = sbuf("y_words", [P, Q], U32)
+        y_scales = sbuf("y_scales", [P, Q], U8)
+        out_rows = out_0.rearrange("(p t) q -> p t q", t=PACK)
+        out_words = out_1[0].rearrange("p c r -> p (c r)").bitcast(I32)
+        y_b = []
+        for j in range(QT):
+            cols = slice(j * P, (j + 1) * P)
+            o_ps = bank("first%d" % j, [P, PACK, P])
+            for t in range(PACK):
+                nc.tensor.matmul_mx(out=o_ps[:, t, :], lhsT=val_codes[t][:].bitcast(FP8X4), lhsT_scale=val_scales[t][:],
+                                    rhs=w_codes[j][:].bitcast(FP8X4), rhs_scale=w_scales[j][:], start=True, stop=True)
+            fresh = sbuf("fresh%d" % j, [P, PACK, P], F32)
+            nc.vector.tensor_tensor(fresh[:], o_ps[:], rest_row[:, cols].unsqueeze(1).to_broadcast([P, PACK, P]), ALU.mult)
+            y = sbuf("y%d" % j, [P, PACK, P], F32)
+            nc.vector.tensor_tensor(y[:], fresh[:], kept[:, :, cols], ALU.add)
+            nc.sync.dma_start(out=out_rows[:, :, cols], in_=y[:])
+            y_b.append(sbuf("y_b%d" % j, [P, P, PACK], BF16))
+            nc.scalar.copy(out=y_b[j][:], in_=y[:].rearrange("p t q -> p q t"))
+        for j in range(QT):
+            cols = slice(j * P, (j + 1) * P)
+            nc.vector.quantize_mx(out=y_words[:, cols].bitcast(FP8X4), scales=y_scales[:, cols],
+                                  in_=y_b[j][:].rearrange("p q t -> p (q t)"))
+            nc.sync.dma_start(out=out_words[:, cols], in_=y_words[:, cols].bitcast(I32))
+        for quad in range(4):
+            engine = nc.scalar if quad % 2 else nc.sync
+            engine.dma_start(out=out_2[0, 4 * quad : 4 * quad + 4, :].bitcast(I32),
+                            in_=y_scales[32 * quad : 32 * quad + 4, :].bitcast(I32))

@@ -33,8 +33,8 @@ def tile_attend_twopools_overlinked_blend_pl_kernel(
         sb = ctx.enter_context(tc.tile_pool(name="sb", bufs=1))
         ps = ctx.enter_context(tc.psum_pool(name="ps", bufs=1))
 
-        def sbuf(name, shape, dtype):
-            return sb.tile(shape, dtype, name=name, align_bytes=64)
+        def sbuf(name, shape, dtype, reuse=None):
+            return sb.tile(shape, dtype, name=name, tag=reuse or name, align_bytes=64)
 
         def bank(tag, shape):
             return ps.tile(shape, F32, name=tag, tag=tag)
@@ -42,17 +42,19 @@ def tile_attend_twopools_overlinked_blend_pl_kernel(
         def half_list(lst, h):
             return lst[:, h * LIST_COLS // 2 : (h + 1) * LIST_COLS // 2]
 
+        def quantize(codes, scales, grouped):
+            nc.vector.quantize_mx(out=codes.bitcast(FP8X4), scales=scales, in_=grouped.rearrange("p c t -> p (c t)"))
+
         key_list = sbuf("key_list", [P, LIST_COLS], U16)
         note_list = sbuf("note_list", [P, LIST_COLS], U16)
         rival_list = sbuf("rival_list", [P, LIST_COLS], U16)
 
         key_scale_pool = sbuf("key_scale_pool", [P, T], U8)
-        nc.vector.memset(key_scale_pool[:].bitcast(I32), 0)
+        nc.gpsimd.memset(key_scale_pool[:].bitcast(I32), 0)
+        vec_rows = sbuf("vec_rows", [P, P], F32)
+        nc.vector.memset(vec_rows[:], 0.0)
         ident = sbuf("ident", [P, P], F32)
         make_identity(nc, ident[:])
-
-        vec_rows = sbuf("vec_rows", [P, P], F32)
-        nc.gpsimd.memset(vec_rows[:], 0.0)
         one = sbuf("one", [P, 1], F32)
         nc.gpsimd.memset(one[:], 1.0)
         mean_factors = sbuf("mean_factors", [P, 2], F32)
@@ -68,52 +70,65 @@ def tile_attend_twopools_overlinked_blend_pl_kernel(
         q2_raw = sbuf("q2_raw", [P, PACK, Q], F32)
         before_sb = sbuf("before_sb", [P, PACK, Q], F32)
 
-        nc.sync.dma_start(note_list[:], offs2)
-        nc.sync.dma_start(out=note_pool[0][:], in_=note_planes[:, 0, :])
-        nc.sync.dma_start(out=note_pool[1][:], in_=note_planes[:, 1, :])
-        for quad in range(4):
+        def load_note_plane(t):
+            nc.sync.dma_start(out=note_pool[t][:], in_=note_planes[:, t, :])
+
+        def load_key_scales(quad):
             nc.sync.dma_start(
                 out=key_scale_pool[32 * quad : 32 * quad + 4, :].bitcast(I32),
                 in_=keys_scales[0, 4 * quad : 4 * quad + 4, :].bitcast(I32),
             )
+
         nc.sync.dma_start(key_list[:], offs)
-        for t in range(2, PACK):
-            nc.sync.dma_start(out=note_pool[t][:], in_=note_planes[:, t, :])
+        nc.sync.dma_start(note_list[:], offs2)
+        nc.sync.dma_start(out=q_raw[:], in_=query.rearrange("(p t) q -> p t q", t=PACK))
+        load_note_plane(0)
+        nc.sync.dma_start(rival_list[:], offs4)
+        for quad in range(4):
+            load_key_scales(quad)
+        for t in range(1, PACK):
+            load_note_plane(t)
         nc.sync.dma_start(out=vec_rows[0:2, :], in_=lam.rearrange("(j p) o -> j (p o)", p=P))
         nc.sync.dma_start(out=vec_rows[2:4, :], in_=rival.rearrange("(j p) o -> j (p o)", p=P))
         nc.sync.dma_start(out=vec_rows[4:6, :], in_=hold.rearrange("o (j p) -> j (o p)", p=P))
         nc.sync.dma_start(out=vec_rows[8:12, :], in_=slot_factor.rearrange("o (j p) -> j (o p)", p=P))
         nc.sync.dma_start(out=key_word_pool[:].bitcast(I32), in_=keys_words[0].bitcast(I32))
-        nc.sync.dma_start(out=q_raw[:], in_=query.rearrange("(p t) q -> p t q", t=PACK))
         nc.sync.dma_start(out=q2_raw[:], in_=query2.rearrange("(p t) q -> p t q", t=PACK))
-        nc.sync.dma_start(rival_list[:], offs4)
-        for t in range(PACK):
-            nc.sync.dma_start(out=val_pool[t][:], in_=val_planes[:, t, :])
+        nc.sync.dma_start(out=val_pool[0][:], in_=val_planes[:, 0, :])
+        nc.sync.dma_start(out=val_pool[1][:], in_=val_planes[:, 1, :])
         nc.sync.dma_start(out=before_sb[:], in_=before.rearrange("(p t) q -> p t q", t=PACK))
+        for t in range(2, PACK):
+            nc.sync.dma_start(out=val_pool[t][:], in_=val_planes[:, t, :])
 
+        def gather(dst, pool, lst, on_vector):
+            if on_vector:
+                nc.vector.tensor_copy(dst, pool[:].indirect(lst))
+            else:
+                nc.scalar.activation(dst, pool[:].indirect(lst), ACT.Copy)
 
-        notes_g = sbuf("notes_g", [P, PACK, I], BF16)
-        nc.scalar.activation(notes_g[:, 0, :], note_pool[0][:].indirect(note_list[:]), ACT.Copy)
-        nc.vector.tensor_copy(notes_g[:, 1, :], note_pool[1][:].indirect(note_list[:]))
+        def group_rows(dst, raw, j, on_vector):
+            src = raw[:].rearrange("p t q -> p q t")[:, j * P : (j + 1) * P, :]
+            if on_vector:
+                nc.vector.tensor_copy(out=dst[:], in_=src)
+            else:
+                nc.scalar.copy(out=dst[:], in_=src)
+
+        q_b = [sbuf("q_b%d" % j, [P, P, PACK], BF16) for j in range(QT)]
+        q_codes = [sbuf("q_codes%d" % j, [P, P], U32) for j in range(QT)]
+        q_scales = [sbuf("q_scales%d" % j, [P, P], U8) for j in range(QT)]
+        for j in range(QT):
+            group_rows(q_b[j], q_raw, j, j == 0)
+        for j in range(QT):
+            quantize(q_codes[j][:], q_scales[j][:], q_b[j][:])
         key_scales = sbuf("key_scales", [P, I], U8)
         nc.vector.tensor_copy(key_scales[:], key_scale_pool[:].indirect(key_list[:]))
-        nc.scalar.activation(notes_g[:, 2, :], note_pool[2][:].indirect(note_list[:]), ACT.Copy)
-        nc.vector.tensor_copy(notes_g[:, 3, 0:HALF], note_pool[3][:].indirect(half_list(note_list, 0)))
-        nc.scalar.activation(notes_g[:, 3, HALF:I], note_pool[3][:].indirect(half_list(note_list, 1)), ACT.Copy)
-        vec_ps = bank("turn0", [P, P])
-        nc.tensor.transpose(vec_ps[:], vec_rows[:], ident[:])
-        vec = sbuf("vec", [P, 12], F32)
-        nc.vector.tensor_copy(out=vec[:], in_=vec_ps[:, 0:12])
-        lam_col = [vec[:, j : j + 1] for j in range(QT)]
-        rival_col = [vec[:, 2 + j : 3 + j] for j in range(QT)]
-        hold_ps = bank("turn1", [P, QT, P])
-        for j in range(QT):
-            nc.tensor.transpose(hold_ps[:, j, :], vec[:, 4 + j : 5 + j].to_broadcast([P, P]), ident[:])
-        os_ps = bank("factor", [P, I // P, P])
-        for c in range(I // P):
-            nc.tensor.transpose(os_ps[:, c, :], vec[:, 8 + c : 9 + c].to_broadcast([P, P]), ident[:])
-        hold_row = sbuf("hold_row", [P, Q], F32)
-        rest_row = sbuf("rest_row", [P, Q], F32)
+
+        notes_g = sbuf("notes_g", [P, PACK, I], BF16)
+        gather(notes_g[:, 0, :], note_pool[0], note_list[:], False)
+        gather(notes_g[:, 1, :], note_pool[1], note_list[:], True)
+        for t in range(2, PACK):
+            for h in range(2):
+                gather(notes_g[:, t, h * HALF : (h + 1) * HALF], note_pool[t], half_list(note_list, h), h == 0)
         notes_b = sbuf("notes_b", [P, I, PACK], BF16)
         notes_t = notes_g[:].rearrange("p t i -> p i t")
         nc.vector.tensor_copy(out=notes_b[:, 0:HALF, :], in_=notes_t[:, 0:HALF, :])
@@ -122,152 +137,176 @@ def tile_attend_twopools_overlinked_blend_pl_kernel(
         nc.vector.tensor_copy(key_words[:], key_word_pool[:].indirect(key_list[:]))
         note_codes = sbuf("note_codes", [P, I], U32)
         note_scales = sbuf("note_scales", [P, I], U8)
-        nc.vector.quantize_mx(out=note_codes[:].bitcast(FP8X4), scales=note_scales[:],
-                              in_=notes_b[:].rearrange("p i t -> p (i t)"))
+        quantize(note_codes[:], note_scales[:], notes_b[:])
 
-        q_b = sbuf("q_b", [P, Q, PACK], BF16)
         q2_b = [sbuf("q2_b%d" % j, [P, P, PACK], BF16) for j in range(QT)]
-        nc.scalar.copy(out=q_b[:], in_=q_raw[:].rearrange("p t q -> p q t"))
-        q2_t = q2_raw[:].rearrange("p t q -> p q t")
-        nc.vector.tensor_copy(out=q2_b[0][:], in_=q2_t[:, 0:P, :])
-        nc.scalar.copy(out=q2_b[1][:], in_=q2_t[:, P:Q, :])
-        q_codes = sbuf("q_codes", [P, Q], U32)
-        q_scales = sbuf("q_scales", [P, Q], U8)
-        nc.vector.quantize_mx(out=q_codes[:].bitcast(FP8X4), scales=q_scales[:],
-                              in_=q_b[:].rearrange("p q t -> p (q t)"))
         q2_codes = [sbuf("q2_codes%d" % j, [P, P], U32) for j in range(QT)]
         q2_scales = [sbuf("q2_scales%d" % j, [P, P], U8) for j in range(QT)]
         for j in range(QT):
-            nc.vector.quantize_mx(out=q2_codes[j][:].bitcast(FP8X4), scales=q2_scales[j][:],
-                                  in_=q2_b[j][:].rearrange("p q t -> p (q t)"))
+            group_rows(q2_b[j], q2_raw, j, False)
+            quantize(q2_codes[j][:], q2_scales[j][:], q2_b[j][:])
 
-        a_ps, b_ps, a_sb = [], [], []
+        vec_ps = bank("turn0", [P, P])
+        nc.tensor.transpose(vec_ps[:], vec_rows[:], ident[:])
+        vec = sbuf("vec", [P, 12], F32)
+        nc.scalar.copy(out=vec[:], in_=vec_ps[:, 0:12])
+        lam_col = [vec[:, j : j + 1] for j in range(QT)]
+        rival_col = [vec[:, 2 + j : 3 + j] for j in range(QT)]
+
+        hold_ps = bank("product0", [P, QT, P])
         for j in range(QT):
-            cols = slice(j * P, (j + 1) * P)
-            a_ps.append(bank("first%d" % j, [P, I]))
+            nc.tensor.transpose(hold_ps[:, j, :], vec[:, 4 + j : 5 + j].to_broadcast([P, P]), ident[:])
+        factor_ps = bank("product1", [P, I // P, P])
+        for c in range(I // P):
+            nc.tensor.transpose(factor_ps[:, c, :], vec[:, 8 + c : 9 + c].to_broadcast([P, P]), ident[:])
+
+        picked = [None] * PACK
+        a_sb = sbuf("a_sb", [P, QT, I], F32, "q2_raw")
+        b_ps = []
+        for j in range(QT):
+            a_ps = bank("first%d" % j, [P, I])
             b_ps.append(bank("second%d" % j, [P, I]))
-            nc.tensor.matmul_mx(out=a_ps[j][:], lhsT=q_codes[:, cols].bitcast(FP8X4), lhsT_scale=q_scales[:, cols],
+            nc.tensor.matmul_mx(out=a_ps[:], lhsT=q_codes[j][:].bitcast(FP8X4), lhsT_scale=q_scales[j][:],
                                 rhs=key_words[:].bitcast(FP4X4), rhs_scale=key_scales[:], start=True, stop=True)
             nc.tensor.matmul_mx(out=b_ps[j][:], lhsT=q2_codes[j][:].bitcast(FP8X4), lhsT_scale=q2_scales[j][:],
                                 rhs=note_codes[:].bitcast(FP8X4), rhs_scale=note_scales[:], start=True, stop=True)
-            a_sb.append(sbuf("a_sb%d" % j, [P, I], F32))
-            nc.scalar.copy(out=a_sb[j][:], in_=a_ps[j][:])
+            nc.scalar.copy(out=a_sb[:, j, :], in_=a_ps[:])
 
+
+        hold_row = sbuf("hold_row", [P, Q], F32, "q2_b0")
+        rest_row = sbuf("rest_row", [P, Q], F32)
         nc.scalar.copy(out=hold_row[:], in_=hold_ps[:].rearrange("p j q -> p (j q)"))
         nc.gpsimd.tensor_scalar(rest_row[:], hold_row[:], -1.0, 1.0, ALU.mult, ALU.add)
-        val_codes = [sbuf("val_codes%d" % t, [P, P], U32) for t in range(PACK)]
-        val_scales = [sbuf("val_scales%d" % t, [P, P], U8) for t in range(PACK)]
-        vals_g = [sbuf("vals_g%d" % t, [P, I], BF16) for t in range(PACK)]
-        vals_b = [sbuf("vals_b%d" % t, [P, P, PACK], BF16) for t in range(PACK)]
 
-        def turn(src, tag, dst):
+        def as_words(grouped):
+            return grouped.rearrange("p c t -> p (c t)").bitcast(F32)
+
+        def turn(src, turned):
             words = src[:].bitcast(F32)
-            turned = bank(tag, [P, 2, P])
             for u in range(2):
                 nc.tensor.transpose(turned[:, u, :], words[:, u : I // 2 : 2], ident[:])
-            nc.scalar.copy(
-                out=dst[:].rearrange("p c t -> p (c t)").bitcast(F32).rearrange("p (c u) -> p c u", u=2),
-                in_=turned[:].rearrange("p u c -> p c u"))
 
-        def gather_vals(t):
-            nc.scalar.activation(vals_g[t][:], val_pool[t][:].indirect(key_list[:]), ACT.Copy)
-            turn(vals_g[t], "turn%d" % (t % 3), vals_b[t])
+        val_turned = [bank("turn%d" % h, [P, 2, 2, P]) for h in range(2)]
+        val_codes = [sbuf("val_codes%d" % h, [P, 2 * P], U32) for h in range(2)]
+        val_scales = [sbuf("val_scales%d" % h, [P, 2 * P], U8) for h in range(2)]
 
-        def quantize_vals(t):
-            nc.vector.quantize_mx(out=val_codes[t][:].bitcast(FP8X4), scales=val_scales[t][:],
-                                  in_=vals_b[t][:].rearrange("p c t -> p (c t)"))
+        def gather_vals(t, on_vector, reuse):
+            picked[t] = sbuf("vals_g%d" % t, [P, I], BF16, reuse)
+            gather(picked[t][:], val_pool[t], key_list[:], on_vector)
+            turn(picked[t], val_turned[t // 2][:, t % 2, :, :])
 
+        def group_vals(h, reuse):
+            grouped = sbuf("vals_b%d" % h, [P, 2 * P, PACK], BF16, reuse)
+            nc.scalar.copy(out=as_words(grouped[:]).rearrange("p (g c u) -> p g c u", g=2, u=2),
+                           in_=val_turned[h][:].rearrange("p g u c -> p g c u"))
+            return grouped
+
+        gather_vals(0, False, "q_codes1")
         p_sb, p_inv = [], []
         for j in range(QT):
+            cols = slice(j * P, (j + 1) * P)
             low = sbuf("low%d" % j, [P, I], F32)
             high = sbuf("high%d" % j, [P, I], F32)
             s = sbuf("s%d" % j, [P, I], F32)
             s_sum = sbuf("s_sum%d" % j, [P, 1], F32)
-            nc.vector.tensor_tensor(low[:], a_sb[j][:], b_ps[j][:], ALU.min)
-            nc.vector.tensor_tensor(high[:], a_sb[j][:], b_ps[j][:], ALU.max)
+            nc.vector.tensor_tensor(low[:], a_sb[:, j, :], b_ps[j][:], ALU.min)
+            nc.vector.tensor_tensor(high[:], a_sb[:, j, :], b_ps[j][:], ALU.max)
             nc.vector.scalar_tensor_tensor(s[:], low[:], lam_col[j], high[:], ALU.mult, ALU.add, accum_out=s_sum[:])
-            if j == 0:
-                gather_vals(0)
             mean = sbuf("mean%d" % j, [P, 2], F32)
             nc.scalar.activation(mean[:], mean_factors[:], ACT.Copy, scale=s_sum[:])
             p_sb.append(sbuf("p%d" % j, [P, I], F32))
             p_inv.append(sbuf("p_inv%d" % j, [P, I], F32))
             nc.scalar.activation(p_sb[j][:], s[:], ACT.Exp, bias=mean[:, 0:1])
             nc.scalar.activation(p_inv[j][:], s[:], ACT.Exp, bias=mean[:, 1:2], scale=-1.0)
+        kept = []
 
-        ratio, positive = [], []
+        def keep(j, reuse):
+            cols = slice(j * P, (j + 1) * P)
+            kept.append(sbuf("kept%d" % j, [P, PACK, P], F32, reuse))
+            nc.gpsimd.tensor_tensor(kept[j][:], before_sb[:, :, cols],
+                                    hold_row[:, cols].unsqueeze(1).to_broadcast([P, PACK, P]), ALU.mult)
+
+        gather_vals(1, True, "low1")
+        keep(0, "high1")
+
+        ratio = []
         for j in range(QT):
             ratio.append(sbuf("ratio%d" % j, [P, I], F32))
             for h in range(2):
                 cols = slice(h * HALF, (h + 1) * HALF)
                 nc.vector.tensor_tensor(ratio[j][:, cols], p_sb[j][:].indirect(half_list(rival_list, h)),
                                         p_inv[j][:, cols], ALU.mult)
-        quantize_vals(0)
-        size = []
+        gather_vals(2, True, "p_inv1")
+        keep(1, "p1")
+        positive, size = [], []
         for j in range(QT):
             positive.append(sbuf("positive%d" % j, [P, I], F32))
             nc.vector.tensor_scalar(positive[j][:], ratio[j][:], rival_col[j], -1.0, ALU.mult, ALU.is_ge)
-            root = sbuf("root%d" % j, [P, I], F32)
+            root = sbuf("root%d" % j, [P, I], F32, "root")
             nc.scalar.activation(root[:], ratio[j][:], ACT.Abs_reciprocal_sqrt, bias=one[:], scale=rival_col[j])
             size.append(sbuf("size%d" % j, [P, I], F32))
             nc.scalar.activation(size[j][:], root[:], ACT.Square)
+            if j == 0:
+                vals_b = [group_vals(0, "ratio0")]
+        gather_vals(3, False, "root")
+        vals_b.append(group_vals(1, None))
 
-        w_b, w_bf = [], []
+        part = [sbuf("part%d" % j, [P, I], F32) for j in range(QT)]
+        part_sum = sbuf("part_sum", [P, QT], F32)
+        part_inv = sbuf("part_inv", [P, QT], F32)
         for j in range(QT):
-            part = sbuf("part%d" % j, [P, I], F32)
-            part_sum = sbuf("part_sum%d" % j, [P, 1], F32)
-            part_inv = sbuf("part_inv%d" % j, [P, 1], F32)
-            nc.vector.scalar_tensor_tensor(part[:], positive[j][:], 0.5, size[j][:], ALU.subtract, ALU.mult,
-                                           accum_out=part_sum[:])
-            nc.vector.reciprocal(part_inv[:], part_sum[:])
-            w_bf.append(sbuf("w_bf%d" % j, [P, I], BF16))
-            nc.vector.scalar_tensor_tensor(w_bf[j][:], part[:], part_inv[:], os_ps[:].rearrange("p c i -> p (c i)"),
-                                           ALU.mult, ALU.mult)
+            nc.vector.scalar_tensor_tensor(part[j][:], positive[j][:], 0.5, size[j][:], ALU.subtract, ALU.mult,
+                                           accum_out=part_sum[:, j : j + 1])
+        nc.vector.reciprocal(part_inv[:], part_sum[:])
+        quantize(val_codes[0][:], val_scales[0][:], vals_b[0][:])
+        w_b = []
+        for j in range(QT):
+            w_bf = sbuf("w_bf%d" % j, [P, I], BF16)
+            nc.vector.scalar_tensor_tensor(w_bf[:], part[j][:], part_inv[:, j : j + 1],
+                                           factor_ps[:].rearrange("p c i -> p (c i)"), ALU.mult, ALU.mult)
+            w_turned = bank("second%d" % j, [P, 2, P])
+            turn(w_bf, w_turned)
             w_b.append(sbuf("w_b%d" % j, [P, P, PACK], BF16))
-        gather_vals(1)
-        turn(w_bf[0], "second0", w_b[0])
-        gather_vals(2)
-        turn(w_bf[1], "second1", w_b[1])
-        gather_vals(3)
-        kept = sbuf("kept", [P, PACK, Q], F32)
-        nc.vector.tensor_tensor(kept[:], before_sb[:], hold_row[:].unsqueeze(1).to_broadcast([P, PACK, Q]), ALU.mult)
-        w_codes = [sbuf("w_codes%d" % j, [P, P], U32) for j in range(QT)]
-        w_scales = [sbuf("w_scales%d" % j, [P, P], U8) for j in range(QT)]
+            nc.scalar.copy(out=as_words(w_b[j][:]).rearrange("p (c u) -> p c u", u=2),
+                           in_=w_turned[:].rearrange("p u c -> p c u"))
 
-        def quantize_w(j):
-            nc.vector.quantize_mx(out=w_codes[j][:].bitcast(FP8X4), scales=w_scales[j][:],
-                                  in_=w_b[j][:].rearrange("p c t -> p (c t)"))
-
-        quantize_vals(1)
-        quantize_w(0)
-        quantize_vals(2)
-        quantize_w(1)
-        quantize_vals(3)
+        quantize(val_codes[1][:], val_scales[1][:], vals_b[1][:])
 
         y_words = sbuf("y_words", [P, Q], U32)
         y_scales = sbuf("y_scales", [P, Q], U8)
         out_rows = out_0.rearrange("(p t) q -> p t q", t=PACK)
         out_words = out_1[0].rearrange("p c r -> p (c r)").bitcast(I32)
+        fresh = []
+        for j in range(QT):
+            cols = slice(j * P, (j + 1) * P)
+            w_codes = sbuf("w_codes%d" % j, [P, P], U32)
+            w_scales = sbuf("w_scales%d" % j, [P, P], U8)
+            quantize(w_codes[:], w_scales[:], w_b[j][:])
+            o_ps = bank("first%d" % j, [P, PACK, P])
+            for t in range(PACK):
+                rows = slice(t % 2 * P, (t % 2 + 1) * P)
+                nc.tensor.matmul_mx(out=o_ps[:, t, :], lhsT=val_codes[t // 2][:, rows].bitcast(FP8X4),
+                                    lhsT_scale=val_scales[t // 2][:, rows],
+                                    rhs=w_codes[:].bitcast(FP8X4), rhs_scale=w_scales[:], start=True, stop=True)
+            fresh.append(sbuf("fresh%d" % j, [P, PACK, P], F32))
+            nc.vector.tensor_tensor(fresh[j][:], o_ps[:], rest_row[:, cols].unsqueeze(1).to_broadcast([P, PACK, P]),
+                                    ALU.mult)
         y_b = []
         for j in range(QT):
             cols = slice(j * P, (j + 1) * P)
-            o_ps = bank("first%d" % j, [P, PACK, P])
-            for t in range(PACK):
-                nc.tensor.matmul_mx(out=o_ps[:, t, :], lhsT=val_codes[t][:].bitcast(FP8X4), lhsT_scale=val_scales[t][:],
-                                    rhs=w_codes[j][:].bitcast(FP8X4), rhs_scale=w_scales[j][:], start=True, stop=True)
-            fresh = sbuf("fresh%d" % j, [P, PACK, P], F32)
-            nc.vector.tensor_tensor(fresh[:], o_ps[:], rest_row[:, cols].unsqueeze(1).to_broadcast([P, PACK, P]), ALU.mult)
             y = sbuf("y%d" % j, [P, PACK, P], F32)
-            nc.vector.tensor_tensor(y[:], fresh[:], kept[:, :, cols], ALU.add)
+            nc.vector.tensor_tensor(y[:], fresh[j][:], kept[j][:], ALU.add)
             nc.sync.dma_start(out=out_rows[:, :, cols], in_=y[:])
             y_b.append(sbuf("y_b%d" % j, [P, P, PACK], BF16))
-            nc.scalar.copy(out=y_b[j][:], in_=y[:].rearrange("p t q -> p q t"))
+            if j == 0:
+                nc.scalar.copy(out=y_b[j][:], in_=y[:].rearrange("p t q -> p q t"))
+            else:
+                nc.vector.tensor_copy(out=y_b[j][:], in_=y[:].rearrange("p t q -> p q t"))
         for j in range(QT):
             cols = slice(j * P, (j + 1) * P)
-            nc.vector.quantize_mx(out=y_words[:, cols].bitcast(FP8X4), scales=y_scales[:, cols],
-                                  in_=y_b[j][:].rearrange("p q t -> p (q t)"))
-            nc.sync.dma_start(out=out_words[:, cols], in_=y_words[:, cols].bitcast(I32))
+            quantize(y_words[:, cols], y_scales[:, cols], y_b[j][:])
+        nc.sync.dma_start(out=out_words, in_=y_words[:].bitcast(I32))
         for quad in range(4):
-            engine = nc.scalar if quad % 2 else nc.sync
+            engine = nc.sync if quad % 2 else nc.scalar
             engine.dma_start(out=out_2[0, 4 * quad : 4 * quad + 4, :].bitcast(I32),
-                            in_=y_scales[32 * quad : 32 * quad + 4, :].bitcast(I32))
+                             in_=y_scales[32 * quad : 32 * quad + 4, :].bitcast(I32))

@@ -51,15 +51,15 @@ def tile_attend_twopools_overlinked_blend_pl_kernel(
 
         key_scale_pool = sbuf("key_scale_pool", [P, T], U8)
         nc.gpsimd.memset(key_scale_pool[:].bitcast(I32), 0)
+        mean_factors = sbuf("mean_factors", [P, 2], F32)
+        nc.vector.memset(mean_factors[:, 0:1], -1.0 / I)
+        nc.scalar.activation(mean_factors[:, 1:2], mean_factors[:, 0:1], ACT.Copy, scale=-1.0)
         vec_rows = sbuf("vec_rows", [P, P], F32)
         nc.vector.memset(vec_rows[:], 0.0)
         ident = sbuf("ident", [P, P], F32)
         make_identity(nc, ident[:])
         one = sbuf("one", [P, 1], F32)
         nc.gpsimd.memset(one[:], 1.0)
-        mean_factors = sbuf("mean_factors", [P, 2], F32)
-        nc.gpsimd.memset(mean_factors[:, 0:1], -1.0 / I)
-        nc.gpsimd.memset(mean_factors[:, 1:2], 1.0 / I)
 
         note_planes = notes.rearrange("(p t) u -> p t u", t=PACK)
         val_planes = vals.rearrange("(p t) n -> p t n", t=PACK)
@@ -81,18 +81,19 @@ def tile_attend_twopools_overlinked_blend_pl_kernel(
 
         nc.sync.dma_start(key_list[:], offs)
         nc.sync.dma_start(note_list[:], offs2)
-        nc.sync.dma_start(out=q_raw[:], in_=query.rearrange("(p t) q -> p t q", t=PACK))
         load_note_plane(0)
+        load_note_plane(1)
         nc.sync.dma_start(rival_list[:], offs4)
         for quad in range(4):
             load_key_scales(quad)
-        for t in range(1, PACK):
+        for t in range(2, PACK):
             load_note_plane(t)
         nc.sync.dma_start(out=vec_rows[0:2, :], in_=lam.rearrange("(j p) o -> j (p o)", p=P))
         nc.sync.dma_start(out=vec_rows[2:4, :], in_=rival.rearrange("(j p) o -> j (p o)", p=P))
         nc.sync.dma_start(out=vec_rows[4:6, :], in_=hold.rearrange("o (j p) -> j (o p)", p=P))
         nc.sync.dma_start(out=vec_rows[8:12, :], in_=slot_factor.rearrange("o (j p) -> j (o p)", p=P))
         nc.sync.dma_start(out=key_word_pool[:].bitcast(I32), in_=keys_words[0].bitcast(I32))
+        nc.sync.dma_start(out=q_raw[:], in_=query.rearrange("(p t) q -> p t q", t=PACK))
         nc.sync.dma_start(out=q2_raw[:], in_=query2.rearrange("(p t) q -> p t q", t=PACK))
         nc.sync.dma_start(out=val_pool[0][:], in_=val_planes[:, 0, :])
         nc.sync.dma_start(out=val_pool[1][:], in_=val_planes[:, 1, :])
@@ -113,19 +114,12 @@ def tile_attend_twopools_overlinked_blend_pl_kernel(
             else:
                 nc.scalar.copy(out=dst[:], in_=src)
 
-        q_b = [sbuf("q_b%d" % j, [P, P, PACK], BF16) for j in range(QT)]
-        q_codes = [sbuf("q_codes%d" % j, [P, P], U32) for j in range(QT)]
-        q_scales = [sbuf("q_scales%d" % j, [P, P], U8) for j in range(QT)]
-        for j in range(QT):
-            group_rows(q_b[j], q_raw, j, j == 0)
-        for j in range(QT):
-            quantize(q_codes[j][:], q_scales[j][:], q_b[j][:])
-        key_scales = sbuf("key_scales", [P, I], U8)
-        nc.vector.tensor_copy(key_scales[:], key_scale_pool[:].indirect(key_list[:]))
 
         notes_g = sbuf("notes_g", [P, PACK, I], BF16)
-        gather(notes_g[:, 0, :], note_pool[0], note_list[:], False)
-        gather(notes_g[:, 1, :], note_pool[1], note_list[:], True)
+        gather(notes_g[:, 0, :], note_pool[0], note_list[:], True)
+        gather(notes_g[:, 1, :], note_pool[1], note_list[:], False)
+        key_scales = sbuf("key_scales", [P, I], U8)
+        nc.vector.tensor_copy(key_scales[:], key_scale_pool[:].indirect(key_list[:]))
         for t in range(2, PACK):
             for h in range(2):
                 gather(notes_g[:, t, h * HALF : (h + 1) * HALF], note_pool[t], half_list(note_list, h), h == 0)
@@ -139,12 +133,18 @@ def tile_attend_twopools_overlinked_blend_pl_kernel(
         note_scales = sbuf("note_scales", [P, I], U8)
         quantize(note_codes[:], note_scales[:], notes_b[:])
 
-        q2_b = [sbuf("q2_b%d" % j, [P, P, PACK], BF16) for j in range(QT)]
-        q2_codes = [sbuf("q2_codes%d" % j, [P, P], U32) for j in range(QT)]
-        q2_scales = [sbuf("q2_scales%d" % j, [P, P], U8) for j in range(QT)]
+        q_codes, q_scales, q2_codes, q2_scales = [], [], [], []
         for j in range(QT):
-            group_rows(q2_b[j], q2_raw, j, False)
-            quantize(q2_codes[j][:], q2_scales[j][:], q2_b[j][:])
+            q_b = sbuf("q_b%d" % j, [P, P, PACK], BF16)
+            q2_b = sbuf("q2_b%d" % j, [P, P, PACK], BF16)
+            q_codes.append(sbuf("q_codes%d" % j, [P, P], U32, "q2_b0" if j else None))
+            q_scales.append(sbuf("q_scales%d" % j, [P, P], U8))
+            q2_codes.append(sbuf("q2_codes%d" % j, [P, P], U32))
+            q2_scales.append(sbuf("q2_scales%d" % j, [P, P], U8))
+            group_rows(q_b, q_raw, j, False)
+            quantize(q_codes[j][:], q_scales[j][:], q_b[:])
+            group_rows(q2_b, q2_raw, j, j == 0)
+            quantize(q2_codes[j][:], q2_scales[j][:], q2_b[:])
 
         vec_ps = bank("turn0", [P, P])
         nc.tensor.transpose(vec_ps[:], vec_rows[:], ident[:])
@@ -173,7 +173,7 @@ def tile_attend_twopools_overlinked_blend_pl_kernel(
             nc.scalar.copy(out=a_sb[:, j, :], in_=a_ps[:])
 
 
-        hold_row = sbuf("hold_row", [P, Q], F32, "q2_b0")
+        hold_row = sbuf("hold_row", [P, Q], F32, "q_scales1")
         rest_row = sbuf("rest_row", [P, Q], F32)
         nc.scalar.copy(out=hold_row[:], in_=hold_ps[:].rearrange("p j q -> p (j q)"))
         nc.gpsimd.tensor_scalar(rest_row[:], hold_row[:], -1.0, 1.0, ALU.mult, ALU.add)
@@ -201,7 +201,7 @@ def tile_attend_twopools_overlinked_blend_pl_kernel(
                            in_=val_turned[h][:].rearrange("p g u c -> p g c u"))
             return grouped
 
-        gather_vals(0, False, "q_codes1")
+        gather_vals(0, False, "q2_b0")
         p_sb, p_inv = [], []
         for j in range(QT):
             cols = slice(j * P, (j + 1) * P)

@@ -17,9 +17,13 @@ ACT = mybir.ActivationFunctionType
 D, T, I, Q, E, U = 512, 2048, 512, 256, 512, 1024
 P = 128
 PACK = 4
-QT = Q // P
+QUADRANTS = 4
+Q_TILES = Q // P
 HALF = I // 2
 LIST_COLS = I // 16
+RUN = 4
+
+LAM_ROW, RIVAL_ROW, HOLD_ROW, FACTOR_ROW, VEC_ROWS = 0, 2, 4, 8, 12
 
 FLOPS = 2 * D * Q * I * 2 + 2 * I * E * Q
 
@@ -39,11 +43,39 @@ def tile_attend_twopools_overlinked_blend_pl_kernel(
         def bank(tag, shape):
             return ps.tile(shape, F32, name=tag, tag=tag)
 
-        def half_list(lst, h):
-            return lst[:, h * LIST_COLS // 2 : (h + 1) * LIST_COLS // 2]
+        def half_list(lst, half):
+            return lst[:, half * LIST_COLS // 2 : (half + 1) * LIST_COLS // 2]
+
+        def q_cols(j):
+            return slice(j * P, (j + 1) * P)
+
+        def slot_cols(half):
+            return slice(half * HALF, (half + 1) * HALF)
 
         def quantize(codes, scales, grouped):
             nc.vector.quantize_mx(out=codes.bitcast(FP8X4), scales=scales, in_=grouped.rearrange("p c t -> p (c t)"))
+
+        def gather(dst, pool, lst, on_vector):
+            if on_vector:
+                nc.vector.tensor_copy(dst, pool[:].indirect(lst))
+            else:
+                nc.scalar.activation(dst, pool[:].indirect(lst), ACT.Copy)
+
+        def group(dst, planes, on_vector):
+            out = dst.rearrange("p (c n) t -> p c t n", n=RUN)
+            src = planes.rearrange("p t (c n) -> p c t n", n=RUN)
+            if on_vector:
+                nc.vector.tensor_copy(out=out, in_=src)
+            else:
+                nc.scalar.copy(out=out, in_=src)
+
+        def as_words(grouped):
+            return grouped.rearrange("p c t -> p (c t)").bitcast(F32)
+
+        def turn(src, turned):
+            words = src[:].bitcast(F32)
+            for u in range(2):
+                nc.tensor.transpose(turned[:, u, :], words[:, u : I // 2 : 2], ident[:])
 
         key_list = sbuf("key_list", [P, LIST_COLS], U16)
         note_list = sbuf("note_list", [P, LIST_COLS], U16)
@@ -70,100 +102,80 @@ def tile_attend_twopools_overlinked_blend_pl_kernel(
         q2_raw = sbuf("q2_raw", [P, PACK, Q], F32)
         before_sb = sbuf("before_sb", [P, PACK, Q], F32)
 
-        def load_note_plane(t):
+        nc.sync.dma_start(key_list[:], offs)
+        nc.sync.dma_start(note_list[:], offs2)
+        for t in range(2):
             nc.sync.dma_start(out=note_pool[t][:], in_=note_planes[:, t, :])
-
-        def load_key_scales(quad):
+        nc.sync.dma_start(rival_list[:], offs4)
+        for quad in range(QUADRANTS):
             nc.sync.dma_start(
                 out=key_scale_pool[32 * quad : 32 * quad + 4, :].bitcast(I32),
                 in_=keys_scales[0, 4 * quad : 4 * quad + 4, :].bitcast(I32),
             )
-
-        nc.sync.dma_start(key_list[:], offs)
-        nc.sync.dma_start(note_list[:], offs2)
-        load_note_plane(0)
-        load_note_plane(1)
-        nc.sync.dma_start(rival_list[:], offs4)
-        for quad in range(4):
-            load_key_scales(quad)
         for t in range(2, PACK):
-            load_note_plane(t)
-        nc.sync.dma_start(out=vec_rows[0:2, :], in_=lam.rearrange("(j p) o -> j (p o)", p=P))
-        nc.sync.dma_start(out=vec_rows[2:4, :], in_=rival.rearrange("(j p) o -> j (p o)", p=P))
-        nc.sync.dma_start(out=vec_rows[4:6, :], in_=hold.rearrange("o (j p) -> j (o p)", p=P))
-        nc.sync.dma_start(out=vec_rows[8:12, :], in_=slot_factor.rearrange("o (j p) -> j (o p)", p=P))
+            nc.sync.dma_start(out=note_pool[t][:], in_=note_planes[:, t, :])
+        nc.sync.dma_start(out=vec_rows[LAM_ROW : LAM_ROW + Q_TILES, :], in_=lam.rearrange("(j p) o -> j (p o)", p=P))
+        nc.sync.dma_start(out=vec_rows[RIVAL_ROW : RIVAL_ROW + Q_TILES, :],
+                          in_=rival.rearrange("(j p) o -> j (p o)", p=P))
+        nc.sync.dma_start(out=vec_rows[HOLD_ROW : HOLD_ROW + Q_TILES, :], in_=hold.rearrange("o (j p) -> j (o p)", p=P))
+        nc.sync.dma_start(out=vec_rows[FACTOR_ROW:VEC_ROWS, :], in_=slot_factor.rearrange("o (j p) -> j (o p)", p=P))
         nc.sync.dma_start(out=key_word_pool[:].bitcast(I32), in_=keys_words[0].bitcast(I32))
         nc.sync.dma_start(out=q_raw[:], in_=query.rearrange("(p t) q -> p t q", t=PACK))
         nc.sync.dma_start(out=q2_raw[:], in_=query2.rearrange("(p t) q -> p t q", t=PACK))
-        nc.sync.dma_start(out=val_pool[0][:], in_=val_planes[:, 0, :])
-        nc.sync.dma_start(out=val_pool[1][:], in_=val_planes[:, 1, :])
+        for t in range(2):
+            nc.sync.dma_start(out=val_pool[t][:], in_=val_planes[:, t, :])
         nc.sync.dma_start(out=before_sb[:], in_=before.rearrange("(p t) q -> p t q", t=PACK))
         for t in range(2, PACK):
             nc.sync.dma_start(out=val_pool[t][:], in_=val_planes[:, t, :])
 
-        def gather(dst, pool, lst, on_vector):
-            if on_vector:
-                nc.vector.tensor_copy(dst, pool[:].indirect(lst))
-            else:
-                nc.scalar.activation(dst, pool[:].indirect(lst), ACT.Copy)
-
-        def group_rows(dst, raw, j, on_vector):
-            src = raw[:].rearrange("p t q -> p q t")[:, j * P : (j + 1) * P, :]
-            if on_vector:
-                nc.vector.tensor_copy(out=dst[:], in_=src)
-            else:
-                nc.scalar.copy(out=dst[:], in_=src)
-
-
         notes_g = sbuf("notes_g", [P, PACK, I], BF16)
-        gather(notes_g[:, 0, :], note_pool[0], note_list[:], True)
-        gather(notes_g[:, 1, :], note_pool[1], note_list[:], False)
+        gather(notes_g[:, 0, :], note_pool[0], note_list[:], on_vector=True)
+        gather(notes_g[:, 1, :], note_pool[1], note_list[:], on_vector=False)
         key_scales = sbuf("key_scales", [P, I], U8)
-        nc.vector.tensor_copy(key_scales[:], key_scale_pool[:].indirect(key_list[:]))
+        gather(key_scales[:], key_scale_pool, key_list[:], on_vector=True)
         for t in range(2, PACK):
-            for h in range(2):
-                gather(notes_g[:, t, h * HALF : (h + 1) * HALF], note_pool[t], half_list(note_list, h), h == 0)
+            for half in range(2):
+                gather(notes_g[:, t, slot_cols(half)], note_pool[t], half_list(note_list, half), on_vector=half == 0)
         notes_b = sbuf("notes_b", [P, I, PACK], BF16)
-        notes_t = notes_g[:].rearrange("p t i -> p i t")
-        nc.vector.tensor_copy(out=notes_b[:, 0:HALF, :], in_=notes_t[:, 0:HALF, :])
-        nc.scalar.copy(out=notes_b[:, HALF:I, :], in_=notes_t[:, HALF:I, :])
+        for half in range(2):
+            group(notes_b[:, slot_cols(half), :], notes_g[:, :, slot_cols(half)], on_vector=half == 0)
         key_words = sbuf("key_words", [P, I], U16)
-        nc.vector.tensor_copy(key_words[:], key_word_pool[:].indirect(key_list[:]))
+        gather(key_words[:], key_word_pool, key_list[:], on_vector=True)
         note_codes = sbuf("note_codes", [P, I], U32)
         note_scales = sbuf("note_scales", [P, I], U8)
         quantize(note_codes[:], note_scales[:], notes_b[:])
 
         q_codes, q_scales, q2_codes, q2_scales = [], [], [], []
-        for j in range(QT):
+        for j in range(Q_TILES):
             q_b = sbuf("q_b%d" % j, [P, P, PACK], BF16)
             q2_b = sbuf("q2_b%d" % j, [P, P, PACK], BF16)
-            q_codes.append(sbuf("q_codes%d" % j, [P, P], U32, "q2_b0" if j else None))
+            q_codes.append(sbuf("q_codes%d" % j, [P, P], U32, reuse="q2_b0" if j else None))
             q_scales.append(sbuf("q_scales%d" % j, [P, P], U8))
             q2_codes.append(sbuf("q2_codes%d" % j, [P, P], U32))
             q2_scales.append(sbuf("q2_scales%d" % j, [P, P], U8))
-            group_rows(q_b, q_raw, j, False)
+            group(q_b[:], q_raw[:, :, q_cols(j)], on_vector=False)
             quantize(q_codes[j][:], q_scales[j][:], q_b[:])
-            group_rows(q2_b, q2_raw, j, j == 0)
+            group(q2_b[:], q2_raw[:, :, q_cols(j)], on_vector=j == 0)
             quantize(q2_codes[j][:], q2_scales[j][:], q2_b[:])
 
         vec_ps = bank("turn0", [P, P])
         nc.tensor.transpose(vec_ps[:], vec_rows[:], ident[:])
-        vec = sbuf("vec", [P, 12], F32)
-        nc.scalar.copy(out=vec[:], in_=vec_ps[:, 0:12])
-        lam_col = [vec[:, j : j + 1] for j in range(QT)]
-        rival_col = [vec[:, 2 + j : 3 + j] for j in range(QT)]
+        vec = sbuf("vec", [P, VEC_ROWS], F32)
+        nc.scalar.copy(out=vec[:], in_=vec_ps[:, 0:VEC_ROWS])
+        lam_col = [vec[:, LAM_ROW + j : LAM_ROW + j + 1] for j in range(Q_TILES)]
+        rival_col = [vec[:, RIVAL_ROW + j : RIVAL_ROW + j + 1] for j in range(Q_TILES)]
 
-        hold_ps = bank("product0", [P, QT, P])
-        for j in range(QT):
-            nc.tensor.transpose(hold_ps[:, j, :], vec[:, 4 + j : 5 + j].to_broadcast([P, P]), ident[:])
-        factor_ps = bank("product1", [P, I // P, P])
+        hold_ps = bank("hold", [P, Q_TILES, P])
+        for j in range(Q_TILES):
+            nc.tensor.transpose(hold_ps[:, j, :], vec[:, HOLD_ROW + j : HOLD_ROW + j + 1].to_broadcast([P, P]), ident[:])
+        factor_ps = bank("factor", [P, I // P, P])
         for c in range(I // P):
-            nc.tensor.transpose(factor_ps[:, c, :], vec[:, 8 + c : 9 + c].to_broadcast([P, P]), ident[:])
+            nc.tensor.transpose(factor_ps[:, c, :], vec[:, FACTOR_ROW + c : FACTOR_ROW + c + 1].to_broadcast([P, P]),
+                                ident[:])
 
-        picked = [None] * PACK
-        a_sb = sbuf("a_sb", [P, QT, I], F32, "q2_raw")
+        a_sb = sbuf("a_sb", [P, Q_TILES, I], F32, reuse="q2_raw")
         b_ps = []
-        for j in range(QT):
+        for j in range(Q_TILES):
             a_ps = bank("first%d" % j, [P, I])
             b_ps.append(bank("second%d" % j, [P, I]))
             nc.tensor.matmul_mx(out=a_ps[:], lhsT=q_codes[j][:].bitcast(FP8X4), lhsT_scale=q_scales[j][:],
@@ -172,39 +184,36 @@ def tile_attend_twopools_overlinked_blend_pl_kernel(
                                 rhs=note_codes[:].bitcast(FP8X4), rhs_scale=note_scales[:], start=True, stop=True)
             nc.scalar.copy(out=a_sb[:, j, :], in_=a_ps[:])
 
-
-        hold_row = sbuf("hold_row", [P, Q], F32, "q_scales1")
+        hold_row = sbuf("hold_row", [P, Q], F32, reuse="q_scales1")
         rest_row = sbuf("rest_row", [P, Q], F32)
         nc.scalar.copy(out=hold_row[:], in_=hold_ps[:].rearrange("p j q -> p (j q)"))
         nc.gpsimd.tensor_scalar(rest_row[:], hold_row[:], -1.0, 1.0, ALU.mult, ALU.add)
 
-        def as_words(grouped):
-            return grouped.rearrange("p c t -> p (c t)").bitcast(F32)
-
-        def turn(src, turned):
-            words = src[:].bitcast(F32)
-            for u in range(2):
-                nc.tensor.transpose(turned[:, u, :], words[:, u : I // 2 : 2], ident[:])
-
-        val_turned = [bank("turn%d" % h, [P, 2, 2, P]) for h in range(2)]
-        val_codes = [sbuf("val_codes%d" % h, [P, 2 * P], U32) for h in range(2)]
-        val_scales = [sbuf("val_scales%d" % h, [P, 2 * P], U8) for h in range(2)]
+        val_turned = [bank("turn%d" % pair, [P, 2, 2, P]) for pair in range(2)]
+        val_codes = [sbuf("val_codes%d" % pair, [P, 2 * P], U32) for pair in range(2)]
+        val_scales = [sbuf("val_scales%d" % pair, [P, 2 * P], U8) for pair in range(2)]
 
         def gather_vals(t, on_vector, reuse):
-            picked[t] = sbuf("vals_g%d" % t, [P, I], BF16, reuse)
-            gather(picked[t][:], val_pool[t], key_list[:], on_vector)
-            turn(picked[t], val_turned[t // 2][:, t % 2, :, :])
+            picked = sbuf("vals_g%d" % t, [P, I], BF16, reuse)
+            gather(picked[:], val_pool[t], key_list[:], on_vector)
+            turn(picked, val_turned[t // 2][:, t % 2, :, :])
 
-        def group_vals(h, reuse):
-            grouped = sbuf("vals_b%d" % h, [P, 2 * P, PACK], BF16, reuse)
+        def group_vals(pair, reuse):
+            grouped = sbuf("vals_b%d" % pair, [P, 2 * P, PACK], BF16, reuse)
             nc.scalar.copy(out=as_words(grouped[:]).rearrange("p (g c u) -> p g c u", g=2, u=2),
-                           in_=val_turned[h][:].rearrange("p g u c -> p g c u"))
+                           in_=val_turned[pair][:].rearrange("p g u c -> p g c u"))
             return grouped
 
-        gather_vals(0, False, "q2_b0")
+        def keep(j, reuse):
+            share = sbuf("kept%d" % j, [P, PACK, P], F32, reuse)
+            nc.gpsimd.tensor_tensor(share[:], before_sb[:, :, q_cols(j)],
+                                    hold_row[:, q_cols(j)].unsqueeze(1).to_broadcast([P, PACK, P]), ALU.mult)
+            return share
+
+        gather_vals(0, on_vector=False, reuse="q2_b0")
+
         p_sb, p_inv = [], []
-        for j in range(QT):
-            cols = slice(j * P, (j + 1) * P)
+        for j in range(Q_TILES):
             low = sbuf("low%d" % j, [P, I], F32)
             high = sbuf("high%d" % j, [P, I], F32)
             s = sbuf("s%d" % j, [P, I], F32)
@@ -218,49 +227,44 @@ def tile_attend_twopools_overlinked_blend_pl_kernel(
             p_inv.append(sbuf("p_inv%d" % j, [P, I], F32))
             nc.scalar.activation(p_sb[j][:], s[:], ACT.Exp, bias=mean[:, 0:1])
             nc.scalar.activation(p_inv[j][:], s[:], ACT.Exp, bias=mean[:, 1:2], scale=-1.0)
-        kept = []
 
-        def keep(j, reuse):
-            cols = slice(j * P, (j + 1) * P)
-            kept.append(sbuf("kept%d" % j, [P, PACK, P], F32, reuse))
-            nc.gpsimd.tensor_tensor(kept[j][:], before_sb[:, :, cols],
-                                    hold_row[:, cols].unsqueeze(1).to_broadcast([P, PACK, P]), ALU.mult)
-
-        gather_vals(1, True, "low1")
-        keep(0, "high1")
+        gather_vals(1, on_vector=True, reuse="low1")
+        kept = [keep(0, reuse="high1")]
 
         ratio = []
-        for j in range(QT):
+        for j in range(Q_TILES):
             ratio.append(sbuf("ratio%d" % j, [P, I], F32))
-            for h in range(2):
-                cols = slice(h * HALF, (h + 1) * HALF)
-                nc.vector.tensor_tensor(ratio[j][:, cols], p_sb[j][:].indirect(half_list(rival_list, h)),
-                                        p_inv[j][:, cols], ALU.mult)
-        gather_vals(2, True, "p_inv1")
-        keep(1, "p1")
-        positive, size = [], []
-        for j in range(QT):
+            for half in range(2):
+                nc.vector.tensor_tensor(ratio[j][:, slot_cols(half)], p_sb[j][:].indirect(half_list(rival_list, half)),
+                                        p_inv[j][:, slot_cols(half)], ALU.mult)
+
+        gather_vals(2, on_vector=True, reuse="p_inv1")
+        kept.append(keep(1, reuse="p1"))
+
+        positive, size, vals_b = [], [], []
+        for j in range(Q_TILES):
             positive.append(sbuf("positive%d" % j, [P, I], F32))
             nc.vector.tensor_scalar(positive[j][:], ratio[j][:], rival_col[j], -1.0, ALU.mult, ALU.is_ge)
-            root = sbuf("root%d" % j, [P, I], F32, "root")
+            root = sbuf("root%d" % j, [P, I], F32, reuse="root")
             nc.scalar.activation(root[:], ratio[j][:], ACT.Abs_reciprocal_sqrt, bias=one[:], scale=rival_col[j])
             size.append(sbuf("size%d" % j, [P, I], F32))
             nc.scalar.activation(size[j][:], root[:], ACT.Square)
             if j == 0:
-                vals_b = [group_vals(0, "ratio0")]
-        gather_vals(3, False, "root")
-        vals_b.append(group_vals(1, None))
+                vals_b.append(group_vals(0, reuse="ratio0"))
 
-        part = [sbuf("part%d" % j, [P, I], F32) for j in range(QT)]
-        part_sum = sbuf("part_sum", [P, QT], F32)
-        part_inv = sbuf("part_inv", [P, QT], F32)
-        for j in range(QT):
+        gather_vals(3, on_vector=False, reuse="root")
+        vals_b.append(group_vals(1, reuse=None))
+
+        part = [sbuf("part%d" % j, [P, I], F32) for j in range(Q_TILES)]
+        part_sum = sbuf("part_sum", [P, Q_TILES], F32)
+        part_inv = sbuf("part_inv", [P, Q_TILES], F32)
+        for j in range(Q_TILES):
             nc.vector.scalar_tensor_tensor(part[j][:], positive[j][:], 0.5, size[j][:], ALU.subtract, ALU.mult,
                                            accum_out=part_sum[:, j : j + 1])
         nc.vector.reciprocal(part_inv[:], part_sum[:])
         quantize(val_codes[0][:], val_scales[0][:], vals_b[0][:])
         w_b = []
-        for j in range(QT):
+        for j in range(Q_TILES):
             w_bf = sbuf("w_bf%d" % j, [P, I], BF16)
             nc.vector.scalar_tensor_tensor(w_bf[:], part[j][:], part_inv[:, j : j + 1],
                                            factor_ps[:].rearrange("p c i -> p (c i)"), ALU.mult, ALU.mult)
@@ -269,7 +273,6 @@ def tile_attend_twopools_overlinked_blend_pl_kernel(
             w_b.append(sbuf("w_b%d" % j, [P, P, PACK], BF16))
             nc.scalar.copy(out=as_words(w_b[j][:]).rearrange("p (c u) -> p c u", u=2),
                            in_=w_turned[:].rearrange("p u c -> p c u"))
-
         quantize(val_codes[1][:], val_scales[1][:], vals_b[1][:])
 
         y_words = sbuf("y_words", [P, Q], U32)
@@ -277,36 +280,30 @@ def tile_attend_twopools_overlinked_blend_pl_kernel(
         out_rows = out_0.rearrange("(p t) q -> p t q", t=PACK)
         out_words = out_1[0].rearrange("p c r -> p (c r)").bitcast(I32)
         fresh = []
-        for j in range(QT):
-            cols = slice(j * P, (j + 1) * P)
+        for j in range(Q_TILES):
             w_codes = sbuf("w_codes%d" % j, [P, P], U32)
             w_scales = sbuf("w_scales%d" % j, [P, P], U8)
             quantize(w_codes[:], w_scales[:], w_b[j][:])
             o_ps = bank("first%d" % j, [P, PACK, P])
             for t in range(PACK):
-                rows = slice(t % 2 * P, (t % 2 + 1) * P)
-                nc.tensor.matmul_mx(out=o_ps[:, t, :], lhsT=val_codes[t // 2][:, rows].bitcast(FP8X4),
-                                    lhsT_scale=val_scales[t // 2][:, rows],
+                plane_cols = slice(t % 2 * P, (t % 2 + 1) * P)
+                nc.tensor.matmul_mx(out=o_ps[:, t, :], lhsT=val_codes[t // 2][:, plane_cols].bitcast(FP8X4),
+                                    lhsT_scale=val_scales[t // 2][:, plane_cols],
                                     rhs=w_codes[:].bitcast(FP8X4), rhs_scale=w_scales[:], start=True, stop=True)
             fresh.append(sbuf("fresh%d" % j, [P, PACK, P], F32))
-            nc.vector.tensor_tensor(fresh[j][:], o_ps[:], rest_row[:, cols].unsqueeze(1).to_broadcast([P, PACK, P]),
-                                    ALU.mult)
+            nc.vector.tensor_tensor(fresh[j][:], o_ps[:],
+                                    rest_row[:, q_cols(j)].unsqueeze(1).to_broadcast([P, PACK, P]), ALU.mult)
         y_b = []
-        for j in range(QT):
-            cols = slice(j * P, (j + 1) * P)
+        for j in range(Q_TILES):
             y = sbuf("y%d" % j, [P, PACK, P], F32)
             nc.vector.tensor_tensor(y[:], fresh[j][:], kept[j][:], ALU.add)
-            nc.sync.dma_start(out=out_rows[:, :, cols], in_=y[:])
+            nc.sync.dma_start(out=out_rows[:, :, q_cols(j)], in_=y[:])
             y_b.append(sbuf("y_b%d" % j, [P, P, PACK], BF16))
-            if j == 0:
-                nc.scalar.copy(out=y_b[j][:], in_=y[:].rearrange("p t q -> p q t"))
-            else:
-                nc.vector.tensor_copy(out=y_b[j][:], in_=y[:].rearrange("p t q -> p q t"))
-        for j in range(QT):
-            cols = slice(j * P, (j + 1) * P)
-            quantize(y_words[:, cols], y_scales[:, cols], y_b[j][:])
+            group(y_b[j][:], y[:], on_vector=j == Q_TILES - 1)
+        for j in range(Q_TILES):
+            quantize(y_words[:, q_cols(j)], y_scales[:, q_cols(j)], y_b[j][:])
         nc.sync.dma_start(out=out_words, in_=y_words[:].bitcast(I32))
-        for quad in range(4):
+        for quad in range(QUADRANTS):
             engine = nc.sync if quad % 2 else nc.scalar
             engine.dma_start(out=out_2[0, 4 * quad : 4 * quad + 4, :].bitcast(I32),
                              in_=y_scales[32 * quad : 32 * quad + 4, :].bitcast(I32))

from contextlib import ExitStack

import concourse.mybir as mybir
from concourse.masks import make_identity

F32 = mybir.dt.float32
BF16 = mybir.dt.bfloat16
I32 = mybir.dt.int32
U32 = mybir.dt.uint32
U16 = mybir.dt.uint16
U8 = mybir.dt.uint8
FP8X4 = mybir.dt.float8_e4m3fn_x4
FP4X4 = mybir.dt.float4_e2m1fn_x4
ALU = mybir.AluOpType
ACT = mybir.ActivationFunctionType

D, T, I, Q, E, U = 512, 2048, 512, 256, 512, 1024
P = 128
PACK = 4
QUADRANTS = 4
Q_TILES = Q // P
HALF = I // 2
LIST_COLS = I // 16
RUN = 4

LAM_ROW, RIVAL_ROW, HOLD_ROW, FACTOR_ROW, VEC_ROWS = 0, 2, 4, 8, 12

FLOPS = 2 * D * Q * I * 2 + 2 * I * E * Q


def tile_attend_twopools_overlinked_blend_pl_kernel(
    tc, query, keys_words, keys_scales, query2, notes, lam, rival, slot_factor, vals, before, hold,
    offs, offs2, offs4, out_0, out_1, out_2,
):
    nc = tc.nc
    with ExitStack() as ctx:
        sb = ctx.enter_context(tc.tile_pool(name="sb", bufs=1))
        ps = ctx.enter_context(tc.psum_pool(name="ps", bufs=1))

        def sbuf(name, shape, dtype, reuse=None):
            return sb.tile(shape, dtype, name=name, tag=reuse or name, align_bytes=64)

        def bank(tag, shape):
            return ps.tile(shape, F32, name=tag, tag=tag)

        def half_list(lst, half):
            return lst[:, half * LIST_COLS // 2 : (half + 1) * LIST_COLS // 2]

        def q_cols(j):
            return slice(j * P, (j + 1) * P)

        def slot_cols(half):
            return slice(half * HALF, (half + 1) * HALF)

        def quantize(codes, scales, grouped):
            nc.vector.quantize_mx(out=codes.bitcast(FP8X4), scales=scales, in_=grouped.rearrange("p c t -> p (c t)"))

        def gather(dst, pool, lst, on_vector):
            if on_vector:
                nc.vector.tensor_copy(dst, pool[:].indirect(lst))
            else:
                nc.scalar.activation(dst, pool[:].indirect(lst), ACT.Copy)

        def group(dst, planes, on_vector):
            out = dst.rearrange("p (c n) t -> p c t n", n=RUN)
            src = planes.rearrange("p t (c n) -> p c t n", n=RUN)
            if on_vector:
                nc.vector.tensor_copy(out=out, in_=src)
            else:
                nc.scalar.copy(out=out, in_=src)

        def as_words(grouped):
            return grouped.rearrange("p c t -> p (c t)").bitcast(F32)

        def turn(src, turned):
            words = src[:].bitcast(F32)
            for u in range(2):
                nc.tensor.transpose(turned[:, u, :], words[:, u : I // 2 : 2], ident[:])

        key_list = sbuf("key_list", [P, LIST_COLS], U16)
        note_list = sbuf("note_list", [P, LIST_COLS], U16)
        rival_list = sbuf("rival_list", [P, LIST_COLS], U16)

        key_scale_pool = sbuf("key_scale_pool", [P, T], U8)
        nc.gpsimd.memset(key_scale_pool[:].bitcast(I32), 0)
        mean_factors = sbuf("mean_factors", [P, 2], F32)
        nc.vector.memset(mean_factors[:, 0:1], -1.0 / I)
        nc.scalar.activation(mean_factors[:, 1:2], mean_factors[:, 0:1], ACT.Copy, scale=-1.0)
        vec_rows = sbuf("vec_rows", [P, P], F32)
        nc.vector.memset(vec_rows[:], 0.0)
        ident = sbuf("ident", [P, P], F32)
        make_identity(nc, ident[:])
        one = sbuf("one", [P, 1], F32)
        nc.gpsimd.memset(one[:], 1.0)

        note_planes = notes.rearrange("(p t) u -> p t u", t=PACK)
        val_planes = vals.rearrange("(p t) n -> p t n", t=PACK)
        note_pool = [sbuf("note_pool%d" % t, [P, U], F32) for t in range(PACK)]
        val_pool = [sbuf("val_pool%d" % t, [P, T], F32) for t in range(PACK)]
        key_word_pool = sbuf("key_word_pool", [P, T], U16)
        q_raw = sbuf("q_raw", [P, PACK, Q], F32)
        q2_raw = sbuf("q2_raw", [P, PACK, Q], F32)
        before_sb = sbuf("before_sb", [P, PACK, Q], F32)

        nc.sync.dma_start(key_list[:], offs)
        nc.sync.dma_start(note_list[:], offs2)
        for t in range(2):
            nc.sync.dma_start(out=note_pool[t][:], in_=note_planes[:, t, :])
        nc.sync.dma_start(rival_list[:], offs4)
        for quad in range(QUADRANTS):
            nc.sync.dma_start(
                out=key_scale_pool[32 * quad : 32 * quad + 4, :].bitcast(I32),
                in_=keys_scales[0, 4 * quad : 4 * quad + 4, :].bitcast(I32),
            )
        for t in range(2, PACK):
            nc.sync.dma_start(out=note_pool[t][:], in_=note_planes[:, t, :])
        nc.sync.dma_start(out=vec_rows[LAM_ROW : LAM_ROW + Q_TILES, :], in_=lam.rearrange("(j p) o -> j (p o)", p=P))
        nc.sync.dma_start(out=vec_rows[RIVAL_ROW : RIVAL_ROW + Q_TILES, :],
                          in_=rival.rearrange("(j p) o -> j (p o)", p=P))
        nc.sync.dma_start(out=vec_rows[HOLD_ROW : HOLD_ROW + Q_TILES, :], in_=hold.rearrange("o (j p) -> j (o p)", p=P))
        nc.sync.dma_start(out=vec_rows[FACTOR_ROW:VEC_ROWS, :], in_=slot_factor.rearrange("o (j p) -> j (o p)", p=P))
        nc.sync.dma_start(out=key_word_pool[:].bitcast(I32), in_=keys_words[0].bitcast(I32))
        nc.sync.dma_start(out=q_raw[:], in_=query.rearrange("(p t) q -> p t q", t=PACK))
        nc.sync.dma_start(out=q2_raw[:], in_=query2.rearrange("(p t) q -> p t q", t=PACK))
        for t in range(2):
            nc.sync.dma_start(out=val_pool[t][:], in_=val_planes[:, t, :])
        nc.sync.dma_start(out=before_sb[:], in_=before.rearrange("(p t) q -> p t q", t=PACK))
        for t in range(2, PACK):
            nc.sync.dma_start(out=val_pool[t][:], in_=val_planes[:, t, :])

        notes_g = sbuf("notes_g", [P, PACK, I], BF16)
        gather(notes_g[:, 0, :], note_pool[0], note_list[:], on_vector=True)
        gather(notes_g[:, 1, :], note_pool[1], note_list[:], on_vector=False)
        key_scales = sbuf("key_scales", [P, I], U8)
        gather(key_scales[:], key_scale_pool, key_list[:], on_vector=True)
        for t in range(2, PACK):
            for half in range(2):
                gather(notes_g[:, t, slot_cols(half)], note_pool[t], half_list(note_list, half), on_vector=half == 0)
        notes_b = sbuf("notes_b", [P, I, PACK], BF16)
        for half in range(2):
            group(notes_b[:, slot_cols(half), :], notes_g[:, :, slot_cols(half)], on_vector=half == 0)
        key_words = sbuf("key_words", [P, I], U16)
        gather(key_words[:], key_word_pool, key_list[:], on_vector=True)
        note_codes = sbuf("note_codes", [P, I], U32)
        note_scales = sbuf("note_scales", [P, I], U8)
        quantize(note_codes[:], note_scales[:], notes_b[:])

        q_codes, q_scales, q2_codes, q2_scales = [], [], [], []
        for j in range(Q_TILES):
            q_b = sbuf("q_b%d" % j, [P, P, PACK], BF16)
            q2_b = sbuf("q2_b%d" % j, [P, P, PACK], BF16)
            q_codes.append(sbuf("q_codes%d" % j, [P, P], U32, reuse="q2_b0" if j else None))
            q_scales.append(sbuf("q_scales%d" % j, [P, P], U8))
            q2_codes.append(sbuf("q2_codes%d" % j, [P, P], U32))
            q2_scales.append(sbuf("q2_scales%d" % j, [P, P], U8))
            group(q_b[:], q_raw[:, :, q_cols(j)], on_vector=False)
            quantize(q_codes[j][:], q_scales[j][:], q_b[:])
            group(q2_b[:], q2_raw[:, :, q_cols(j)], on_vector=j == 0)
            quantize(q2_codes[j][:], q2_scales[j][:], q2_b[:])

        vec_ps = bank("turn0", [P, P])
        nc.tensor.transpose(vec_ps[:], vec_rows[:], ident[:])
        vec = sbuf("vec", [P, VEC_ROWS], F32)
        nc.scalar.copy(out=vec[:], in_=vec_ps[:, 0:VEC_ROWS])
        lam_col = [vec[:, LAM_ROW + j : LAM_ROW + j + 1] for j in range(Q_TILES)]
        rival_col = [vec[:, RIVAL_ROW + j : RIVAL_ROW + j + 1] for j in range(Q_TILES)]

        hold_ps = bank("hold", [P, Q_TILES, P])
        for j in range(Q_TILES):
            nc.tensor.transpose(hold_ps[:, j, :], vec[:, HOLD_ROW + j : HOLD_ROW + j + 1].to_broadcast([P, P]), ident[:])
        factor_ps = bank("factor", [P, I // P, P])
        for c in range(I // P):
            nc.tensor.transpose(factor_ps[:, c, :], vec[:, FACTOR_ROW + c : FACTOR_ROW + c + 1].to_broadcast([P, P]),
                                ident[:])

        a_sb = sbuf("a_sb", [P, Q_TILES, I], F32, reuse="q2_raw")
        b_ps = []
        for j in range(Q_TILES):
            a_ps = bank("first%d" % j, [P, I])
            b_ps.append(bank("second%d" % j, [P, I]))
            nc.tensor.matmul_mx(out=a_ps[:], lhsT=q_codes[j][:].bitcast(FP8X4), lhsT_scale=q_scales[j][:],
                                rhs=key_words[:].bitcast(FP4X4), rhs_scale=key_scales[:], start=True, stop=True)
            nc.tensor.matmul_mx(out=b_ps[j][:], lhsT=q2_codes[j][:].bitcast(FP8X4), lhsT_scale=q2_scales[j][:],
                                rhs=note_codes[:].bitcast(FP8X4), rhs_scale=note_scales[:], start=True, stop=True)
            nc.scalar.copy(out=a_sb[:, j, :], in_=a_ps[:])

        hold_row = sbuf("hold_row", [P, Q], F32, reuse="q_scales1")
        rest_row = sbuf("rest_row", [P, Q], F32)
        nc.scalar.copy(out=hold_row[:], in_=hold_ps[:].rearrange("p j q -> p (j q)"))
        nc.gpsimd.tensor_scalar(rest_row[:], hold_row[:], -1.0, 1.0, ALU.mult, ALU.add)

        val_turned = [bank("turn%d" % pair, [P, 2, 2, P]) for pair in range(2)]
        val_codes = [sbuf("val_codes%d" % pair, [P, 2 * P], U32) for pair in range(2)]
        val_scales = [sbuf("val_scales%d" % pair, [P, 2 * P], U8) for pair in range(2)]

        def gather_vals(t, on_vector, reuse):
            picked = sbuf("vals_g%d" % t, [P, I], BF16, reuse)
            gather(picked[:], val_pool[t], key_list[:], on_vector)
            turn(picked, val_turned[t // 2][:, t % 2, :, :])

        def group_vals(pair, reuse):
            grouped = sbuf("vals_b%d" % pair, [P, 2 * P, PACK], BF16, reuse)
            nc.scalar.copy(out=as_words(grouped[:]).rearrange("p (g c u) -> p g c u", g=2, u=2),
                           in_=val_turned[pair][:].rearrange("p g u c -> p g c u"))
            return grouped

        def keep(j, reuse):
            share = sbuf("kept%d" % j, [P, PACK, P], F32, reuse)
            nc.gpsimd.tensor_tensor(share[:], before_sb[:, :, q_cols(j)],
                                    hold_row[:, q_cols(j)].unsqueeze(1).to_broadcast([P, PACK, P]), ALU.mult)
            return share

        gather_vals(0, on_vector=False, reuse="q2_b0")

        p_sb, p_inv = [], []
        for j in range(Q_TILES):
            low = sbuf("low%d" % j, [P, I], F32)
            high = sbuf("high%d" % j, [P, I], F32)
            s = sbuf("s%d" % j, [P, I], F32)
            s_sum = sbuf("s_sum%d" % j, [P, 1], F32)
            nc.vector.tensor_tensor(low[:], a_sb[:, j, :], b_ps[j][:], ALU.min)
            nc.vector.tensor_tensor(high[:], a_sb[:, j, :], b_ps[j][:], ALU.max)
            nc.vector.scalar_tensor_tensor(s[:], low[:], lam_col[j], high[:], ALU.mult, ALU.add, accum_out=s_sum[:])
            mean = sbuf("mean%d" % j, [P, 2], F32)
            nc.scalar.activation(mean[:], mean_factors[:], ACT.Copy, scale=s_sum[:])
            p_sb.append(sbuf("p%d" % j, [P, I], F32))
            p_inv.append(sbuf("p_inv%d" % j, [P, I], F32))
            nc.scalar.activation(p_sb[j][:], s[:], ACT.Exp, bias=mean[:, 0:1])
            nc.scalar.activation(p_inv[j][:], s[:], ACT.Exp, bias=mean[:, 1:2], scale=-1.0)

        gather_vals(1, on_vector=True, reuse="low1")
        kept = [keep(0, reuse="high1")]

        ratio = []
        for j in range(Q_TILES):
            ratio.append(sbuf("ratio%d" % j, [P, I], F32))
            for half in range(2):
                nc.vector.tensor_tensor(ratio[j][:, slot_cols(half)], p_sb[j][:].indirect(half_list(rival_list, half)),
                                        p_inv[j][:, slot_cols(half)], ALU.mult)

        gather_vals(2, on_vector=True, reuse="p_inv1")
        kept.append(keep(1, reuse="p1"))

        positive, size, vals_b = [], [], []
        for j in range(Q_TILES):
            positive.append(sbuf("positive%d" % j, [P, I], F32))
            nc.vector.tensor_scalar(positive[j][:], ratio[j][:], rival_col[j], -1.0, ALU.mult, ALU.is_ge)
            root = sbuf("root%d" % j, [P, I], F32, reuse="root")
            nc.scalar.activation(root[:], ratio[j][:], ACT.Abs_reciprocal_sqrt, bias=one[:], scale=rival_col[j])
            size.append(sbuf("size%d" % j, [P, I], F32))
            nc.scalar.activation(size[j][:], root[:], ACT.Square)
            if j == 0:
                vals_b.append(group_vals(0, reuse="ratio0"))

        gather_vals(3, on_vector=False, reuse="root")
        vals_b.append(group_vals(1, reuse=None))

        part = [sbuf("part%d" % j, [P, I], F32) for j in range(Q_TILES)]
        part_sum = sbuf("part_sum", [P, Q_TILES], F32)
        part_inv = sbuf("part_inv", [P, Q_TILES], F32)
        for j in range(Q_TILES):
            nc.vector.scalar_tensor_tensor(part[j][:], positive[j][:], 0.5, size[j][:], ALU.subtract, ALU.mult,
                                           accum_out=part_sum[:, j : j + 1])
        nc.vector.reciprocal(part_inv[:], part_sum[:])
        quantize(val_codes[0][:], val_scales[0][:], vals_b[0][:])
        w_b = []
        for j in range(Q_TILES):
            w_bf = sbuf("w_bf%d" % j, [P, I], BF16)
            nc.vector.scalar_tensor_tensor(w_bf[:], part[j][:], part_inv[:, j : j + 1],
                                           factor_ps[:].rearrange("p c i -> p (c i)"), ALU.mult, ALU.mult)
            w_turned = bank("second%d" % j, [P, 2, P])
            turn(w_bf, w_turned)
            w_b.append(sbuf("w_b%d" % j, [P, P, PACK], BF16))
            nc.scalar.copy(out=as_words(w_b[j][:]).rearrange("p (c u) -> p c u", u=2),
                           in_=w_turned[:].rearrange("p u c -> p c u"))
        quantize(val_codes[1][:], val_scales[1][:], vals_b[1][:])

        y_words = sbuf("y_words", [P, Q], U32)
        y_scales = sbuf("y_scales", [P, Q], U8)
        out_rows = out_0.rearrange("(p t) q -> p t q", t=PACK)
        out_words = out_1[0].rearrange("p c r -> p (c r)").bitcast(I32)
        fresh = []
        for j in range(Q_TILES):
            w_codes = sbuf("w_codes%d" % j, [P, P], U32)
            w_scales = sbuf("w_scales%d" % j, [P, P], U8)
            quantize(w_codes[:], w_scales[:], w_b[j][:])
            o_ps = bank("first%d" % j, [P, PACK, P])
            for t in range(PACK):
                plane_cols = slice(t % 2 * P, (t % 2 + 1) * P)
                nc.tensor.matmul_mx(out=o_ps[:, t, :], lhsT=val_codes[t // 2][:, plane_cols].bitcast(FP8X4),
                                    lhsT_scale=val_scales[t // 2][:, plane_cols],
                                    rhs=w_codes[:].bitcast(FP8X4), rhs_scale=w_scales[:], start=True, stop=True)
            fresh.append(sbuf("fresh%d" % j, [P, PACK, P], F32))
            nc.vector.tensor_tensor(fresh[j][:], o_ps[:],
                                    rest_row[:, q_cols(j)].unsqueeze(1).to_broadcast([P, PACK, P]), ALU.mult)
        y_b = []
        for j in range(Q_TILES):
            y = sbuf("y%d" % j, [P, PACK, P], F32)
            nc.vector.tensor_tensor(y[:], fresh[j][:], kept[j][:], ALU.add)
            nc.sync.dma_start(out=out_rows[:, :, q_cols(j)], in_=y[:])
            y_b.append(sbuf("y_b%d" % j, [P, P, PACK], BF16))
            group(y_b[j][:], y[:], on_vector=j == Q_TILES - 1)
        for j in range(Q_TILES):
            quantize(y_words[:, q_cols(j)], y_scales[:, q_cols(j)], y_b[j][:])
        nc.sync.dma_start(out=out_words, in_=y_words[:].bitcast(I32))
        for quad in range(QUADRANTS):
            engine = nc.sync if quad % 2 else nc.scalar
            engine.dma_start(out=out_2[0, 4 * quad : 4 * quad + 4, :].bitcast(I32),
                             in_=y_scales[32 * quad : 32 * quad + 4, :].bitcast(I32))
